import numpy as np, ml_dtypes
CORES = [9,25,41,57]
N = 4
BF = ml_dtypes.bfloat16
S, U, NP, CAP, FO, RO = 2048, 2048, 192, 64, 1, 5
G = NP + FO * CAP
def parts(rng):
    x = rng.integers(0, 256, (N, 8, 16, S)); kd = rng.integers(0, 4096, (N, 16, U)); wt = rng.integers(0, 256, (N, 8, 16, 1))
    th = rng.integers(64, 208, (N, 8, 16, 1)); th = np.where(rng.random(th.shape) < 0.06, 256 * rng.integers(0, 2, th.shape), th)
    tau = rng.integers(900, 1700, (N, 8, 1, 1)) + rng.integers(-150, 151, (N, 8, 16, 1))
    return x, kd, wt, th, tau
def pack(x, kd, wt, th, tau):
    col = lambda a: np.ascontiguousarray(a.reshape(N, 128, 1)).astype(np.int32)
    return {"x0": np.ascontiguousarray(x.reshape(N, 128, S)).astype(np.float32).astype(BF), "kd": kd.astype(np.int32), "wt": col(wt), "th": col(th), "tau": col(tau)}
def draw_of(a):
    return (a * 4096 + S - 1) // S
def apart(rng, n):
    got = []; used = {0}
    for d in rng.permutation(np.arange(64, 4096 * S // (S + (RO - 1) * G))):
        v = {int(d) * (S + t * G) >> 12 for t in range(RO)}
        if len(v) == RO and not v & used:
            got.append(int(d)); used |= v
        if len(got) == n: break
    return np.array(got)
def columns_of(rng, h):
    z = h[:, None, :] // 16 + (np.arange(16)[None, :, None] < h[:, None, :] % 16)
    a, b = z[:, ::2], z[:, 1::2]; s = rng.integers(0, np.minimum(a, 255 - b) + 1); z = np.concatenate([a - s, b + s], axis=1)
    return np.take_along_axis(z, np.argsort(rng.random(z.shape), axis=1), 1)
def setup_inputs(rng):
    return pack(*parts(rng))
def setup_inputs_corners(rng):
    x, kd, wt, th, tau = parts(rng)
    kd = np.where(rng.random(kd.shape) < 0.3, 4095 * rng.integers(0, 2, kd.shape), kd); ui = (613 * np.arange(NP)) & (U - 1)
    for a in range(N):
        o = 2 + rng.permutation(S - 2); o = np.concatenate([[0], o[:NP - 1], [1], o[NP - 1:]]); p, q = o[:NP], o[NP:2 * NP]
        first = rng.random((16, NP)) < 0.5; first[0] = True; first[15] = False
        kd[a][:, ui] = draw_of(np.where(first, p[None, :], q[None, :]))
        cnt = rng.permutation(np.array([0, 1, CAP - 1, CAP, CAP + 1, NP]))
        for g in range(6):
            m = rng.permutation(NP)[:int(cnt[g])]
            wt[a, g] = 0; th[a, g] = 256 * rng.integers(0, 2, (16, 1)); th[a, g, 0] = 0
            tau[a, g] = rng.choice(np.array([0, 1, 1000, 1500, 4079, 4080]), (16, 1)); tau[a, g, 0] = 4079
            x[a, g][:, q] = x[a, g][:, p]; x[a, g][:, p[m]] = 0; x[a, g][:, q[m]] = 255
        wt[a, 6] = 255; th[a, 6] = rng.choice(np.array([0, 1, 128, 255, 256]), (16, 1)); tau[a, 6] = rng.choice(np.array([0, 1300, 4080]), (16, 1))
        th[a, 7] = 256
    return pack(x, kd, wt, th, tau)
def setup_inputs_deep(rng):
    x, kd, wt, th, tau = parts(rng)
    near = 4095 - np.floor(300 * rng.random(kd.shape) ** 2).astype(np.int64)
    kd = np.where(rng.random(kd.shape) < 0.7, near, kd); th = rng.integers(90, 140, th.shape)
    tau = np.minimum(rng.choice(np.array([0, 300, 600, 900, 1200, 4080]), (N, 8, 1, 1)) + rng.integers(0, 200, (N, 8, 16, 1)), 4080)
    tau[:, 2] = 4080; tau[:, 5] = 0
    return pack(x, kd, wt, th, tau)
def setup_inputs_ends(rng):
    x = 255 * rng.integers(0, 2, (N, 8, 16, S)); x = np.where(rng.random((N, 8, 1, S)) < 0.4, 255 * rng.integers(0, 2, (N, 8, 1, S)), x)
    wt = 255 * rng.integers(0, 2, (N, 8, 16, 1)); sh = wt.shape
    th = np.where(rng.random(sh) < 0.75, 256 * rng.integers(0, 2, sh), rng.choice(np.array([1, 128, 255]), sh))
    tau = np.where(rng.random(sh) < 0.7, 4080 * rng.integers(0, 2, sh), 255 * rng.integers(0, 17, sh))
    end = (rng.random((N, 1, U)) < 0.5) | (rng.random((N, 16, U)) < 0.5)
    kd = np.where(end, 4095 * rng.integers(0, 2, (N, 16, U)), rng.integers(0, 4096, (N, 16, U)))
    bits = rng.integers(0, 2, (N, 1, S)); bits[..., 0] = 0; bits[..., S - 1] = 1; bits[..., S - G] = 1; bits[..., S - G + 1] = 0; bits[..., S - G + NP - 1] = 1
    x[:, 7] = 255 * bits; wt[:, 7] = 255
    th[:, 7] = 256 * rng.integers(0, 2, (N, 16, 1)); th[:, 7, 0] = 0; th[:, 7, 1] = 256; th[:, 7, 14] = 0; th[:, 7, 15] = 0
    tau[:, 7] = 4080 * rng.integers(0, 2, (N, 16, 1)); tau[:, 7, 0] = 4080; tau[:, 7, 14] = 4080; tau[:, 7, 15] = 0
    i = 613 * np.arange(NP); both = np.unique(np.concatenate([i & (U - 1), (i + 16 * 255 * 255) & (U - 1)]))
    kd[:, :, both] = 4095 * rng.integers(0, 2, (N, 16, len(both))); kd[:, 1, both] = 4095; kd[:, 15, both] = 0; kd[:, 0, 0] = 0
    e = np.array([613 * (CAP - 1), 613 * (NP - 1)]); e = np.concatenate([e, e + 16 * 255 * 255]) & (U - 1)
    kd[:, :, e] = 4095; kd[:, 15, e] = 0; kd[:, 0, (e + 1) & (U - 1)] = 4095
    return pack(x, kd, wt, th, tau)
def setup_inputs_spread(rng):
    x, kd, wt, th, tau = parts(rng); sh = wt.shape
    x = np.minimum(np.floor(np.exp2(8 * rng.random((N, 8, 1, S))) * rng.random((N, 8, 16, S))), 255).astype(np.int64)
    kd = np.minimum(np.floor(4096 * rng.random((N, 16, U)) ** np.exp2(rng.integers(-2, 3, (N, 1, U)))), 4095).astype(np.int64)
    wt = np.minimum(np.floor(np.exp2(8 * rng.random(sh))) - 1, 255).astype(np.int64); wt[:, :, 3] = 255
    th = np.where(rng.random(sh) < 0.7, np.minimum(np.floor(np.exp2(8.01 * rng.random(sh))) - 1, 256), rng.integers(0, 257, sh)).astype(np.int64)
    tau = np.where(rng.random(sh) < 0.5, np.minimum(np.floor(np.exp2(12 * rng.random(sh))) - 1, 4080), rng.integers(200, 2200, sh)).astype(np.int64)
    return pack(x, kd, wt, th, tau)
def setup_inputs_turns(rng):
    x, kd, wt, th, tau = parts(rng); wt[...] = 0; ui = (613 * np.arange(NP)) & (U - 1); n = 20; tight = np.arange(n) % 2 == 0
    own = np.concatenate([np.arange(4), np.full(CAP - 2, 4), 5 + np.arange(NP - CAP - 2) % (n - 5)])
    pat = np.zeros((6, n), bool); pat[1, 0] = True; pat[2, [0, 4]] = True; pat[3, [0, 1, 4]] = True; pat[4, [0, 1, 2, 4]] = True; pat[5] = True
    q = rng.permutation(N)
    for a in range(N):
        d = apart(rng, n); c = rng.permutation(own); size = np.bincount(c, minlength=n)
        first = rng.random((16, NP)) < 0.5; first[0] = True; first[15] = False
        kd[a][:, ui] = np.where(first, d[c][None, :], 0)
        opt = rng.integers(0, 7, (RO, 8))
        if a == q[0]:
            opt[0] = rng.permutation(np.array([0, 1, 1, 1, 2, 3, 4, 5])); opt[1] = 0; opt[2] = rng.integers(1, 6, 8)
        if a == q[1]:
            opt[1] = 5; opt[2] = rng.integers(1, 6, 8)
        go = np.where((opt == 6)[..., None], rng.random((RO, 8, n)) < 0.5, pat[np.minimum(opt, 5)])
        least = rng.permutation(np.concatenate([np.array([0, 64, 2047, 2048, 4064]), rng.integers(100, 4065, 3)])); row = rng.integers(0, 16, 8)
        th[a, :, :, 0] = rng.choice(np.array([0, 0, 1, 128, 255, 256]), (8, 16))
        tau[a, :, :, 0] = np.minimum(least[:, None] + rng.choice(np.array([0, 0, 1, 15, 500, 4080]), (8, 16)), 4080)
        th[a, np.arange(8), row, 0] = 0; tau[a, np.arange(8), row, 0] = least
        count = 0
        for t in range(RO):
            lim = (least + (count & 15))[:, None]; v = (d * (S + t * G)) >> 12
            over = np.where(tight, 1, 1 + np.floor((4080 - lim) * rng.random((8, n))).astype(np.int64))
            under = np.where(tight, 0, np.floor((lim + 1) * rng.random((8, n))).astype(np.int64))
            x[a][:, :, v] = columns_of(rng, np.where(go[t], lim + over, lim - under))
            count = int(np.sum(size * go[t]))
        x[a][:, :, 0] = 0
    return pack(x, kd, wt, th, tau)
def check_inputs(d):
    bad = []
    for k, lo, hi in (("x0", 0, 255), ("kd", 0, 4095), ("wt", 0, 255), ("th", 0, 256), ("tau", 0, 4080)):
        a = np.asarray(d[k]).astype(np.float64)
        if not (np.all(a >= lo) and np.all(a <= hi) and np.all(a == np.floor(a))): bad.append("range of " + k)
    return bad
def reference(x0, kd, wt, th, tau):
    tot = S + RO * G
    X = np.zeros((N, 8, 16, tot), np.int64); X[..., :S] = x0.astype(np.float32).astype(np.int64).reshape(N, 8, 16, S)
    A = np.zeros((N, 8, 16, tot), np.int64); A[...] = np.arange(tot)
    tb = kd.astype(np.int64); w = wt.astype(np.int64).reshape(N, 8, 16, 1); lim = tau.astype(np.int64).reshape(N, 8, 16, 1); thr = th.astype(np.int64).reshape(N, 8, 16, 1, 1)
    C = [0] * N
    for t in range(RO):
        B = S + t * G
        u = (np.sum(w * X[..., B - G:B - G + NP], axis=2) + 613 * np.arange(NP)) & (U - 1)
        mail = []
        for a in range(N):
            e = (tb[a][:, u[a]] * B) >> 12
            ix = np.ascontiguousarray(e.transpose(1, 2, 0)).reshape(8, 1, NP * 16)
            xe = np.take_along_axis(X[a], ix, 2).reshape(8, 16, NP, 16); ne = np.take_along_axis(A[a], ix, 2).reshape(8, 16, NP, 16)
            m = xe >= thr[a]
            lo = np.min(np.where(m, ne, tot), axis=3); hi = np.max(np.where(m, ne, -1), axis=3); none = hi < 0
            lo = np.where(none, ne[..., 0], lo); hi = np.where(none, ne[..., 0], hi)
            xl = np.take_along_axis(X[a], lo.reshape(8, 1, 16 * NP), 2).reshape(8, 16, 16, NP)
            xh = np.take_along_axis(X[a], hi.reshape(8, 1, 16 * NP), 2).reshape(8, 16, 16, NP)
            D = np.sum(np.abs(xl - xh), axis=1)
            far = D > lim[a] + (C[a] & 15)
            A[a, :, :, B:B + NP] = np.where(far, np.arange(B, B + NP), lo)
            nx = (np.max(xl, axis=2) + np.min(xh, axis=2)) >> 1
            X[a, :, :, B:B + NP] = nx
            c = np.any(far, axis=1)
            C[a] = int(np.sum(c))
            o = np.argsort(np.where(c, 0, 1), axis=1, kind="stable")[:, :CAP]
            mail.append(np.where(np.take_along_axis(c, o, 1)[:, None, :], np.take_along_axis(nx, o[:, None, :], 2), 0))
        for a in range(N):
            for f in range(FO):
                q = (a - 1 - (FO * t + f) % (N - 1)) % N; b = B + NP + f * CAP
                X[a, :, :, b:b + CAP] = mail[q]
    return {"ya": A[..., S:].reshape(N, 128, RO * G).astype(np.float32), "yx": X[..., S:].reshape(N, 128, RO * G).astype(np.float32).astype(BF)}

@@ -1,0 +1,457 @@
+import math
+from concourse.mybir import dt, AluOpType, AxisListType, ActivationFunctionType
+
+S, NP, CAP, RO, G = 2048, 192, 64, 5, 256
+TOT = S + RO * G
+CH = [(0, 64), (64, 64), (128, 64)]
+SG = [[0, 1, 2]]
+GE = {"Vxh1": "S", "Vxl2": "S", "Vgk2": "S", "Vxl0": "S"}
+PRI = {"Vf0p": 3, "Vf0s2": 12, "Vs0": 12, "Vsf": 6, "Slh0": 1.5, "VTM": 6, "Sga1": 12, "Vnrm0": -1.5, "Ve32": -1.5, "Vf0s1": -1.5,
+       "VW1s0": 1.5, "VsM1": -3, "VsM0": -6, "VZW": -1.5, "Vs613": 12}
+DV = [(2, 1)]
+NCH = len(CH)
+WIDE = 16 * max(n for _, n in CH)
+LASTN = sum(CH[c][1] for c in SG[-1])
+N0 = 2590
+H = 63 * math.log(2.0) / N0
+WB = 81
+PLAIN = 2.0 ** 99
+FAR = 9.0e29
+MW = 1152
+MAGIC = 8388608.0
+
+SCRATCH = {
+    "X": ("sbuf", [128, TOT], "bfloat16"),
+    "W": ("sbuf", [128, 2 * TOT], "bfloat16"),
+    "kdw": ("sbuf", [128, 2048], "int32"),
+    "nam": ("sbuf", [128, 512], "float32"),
+    "A": ("sbuf", [128, RO * G], "float32"),
+    "en": ("sbuf", [128, RO * G], "bfloat16"),
+    "f0s": ("sbuf", [128, 2048], "bfloat16"),
+    "f1s": ("sbuf", [128, 2048], "bfloat16"),
+    "f0": ("sbuf", [128, 256], "bfloat16"),
+    "ng": ("sbuf", [128, RO * G], "bfloat16"),
+    "gk": ("sbuf", [128, 3072], "bfloat16"),
+    "ga": ("sbuf", [128, 3072], "bfloat16"),
+    "sM": ("sbuf", [128, 3072], "bfloat16"),
+    "sm": ("sbuf", [128, 3072], "bfloat16"),
+    "xl": ("sbuf", [128, 3072], "bfloat16"),
+    "xh": ("sbuf", [128, 3072], "bfloat16"),
+    "sl": ("sbuf", [128, 3072], "bfloat16"),
+    "sh": ("sbuf", [128, 3072], "bfloat16"),
+    "df": ("sbuf", [128, 3072], "bfloat16"),
+    "da": ("sbuf", [128, 3072], "bfloat16"),
+    "rmax": ("sbuf", [128, WIDE], "bfloat16"),
+    "rmin": ("sbuf", [128, WIDE], "bfloat16"),
+    "nrm": ("sbuf", [128, 192], "bfloat16"),
+    "loc": ("sbuf", [128, 192], "bfloat16"),
+    "hic": ("sbuf", [128, 192], "bfloat16"),
+    "lh": ("sbuf", [128, 384], "float32"),
+    "LH": ("sbuf", [128, 384], "uint16"),
+    "ln1": ("sbuf", [128, 192], "float32"),
+    "ln2": ("sbuf", [128, 192], "float32"),
+    "EL": ("sbuf", [128, 192], "uint16"),
+    "e32": ("sbuf", [128, 192], "int32"),
+    "far": ("sbuf", [128, 192], "bfloat16"),
+    "fn": ("sbuf", [128, 192], "bfloat16"),
+    "cm": ("sbuf", [128, LASTN], "bfloat16"),
+    "cs": ("sbuf", [128, LASTN], "bfloat16"),
+    "msk": ("sbuf", [128, LASTN], "bfloat16"),
+    "mio": ("sbuf", [128, LASTN], "float32"),
+    "UL": ("sbuf", [128, 16], "uint16"),
+    "u1": ("sbuf", [128, 16], "int32"),
+    "u2": ("sbuf", [128, 16], "int32"),
+    "k613": ("sbuf", [128, 16], "float32"),
+    "ki": ("sbuf", [128, 16], "int32"),
+    "kj": ("sbuf", [128, 16], "int32"),
+    "kl": ("sbuf", [128, 16], "int32"),
+    "wi": ("sbuf", [128, 16], "float32"),
+    "wc": ("sbuf", [128, 16], "bfloat16"),
+    "Fb": ("sbuf", [128, 16], "bfloat16"),
+    "inc": ("sbuf", [128, 16], "bfloat16"),
+    "Fw": ("sbuf", [128, 16], "bfloat16"),
+    "slots": ("sbuf", [128, 16], "uint16"),
+    "z12": ("sbuf", [128, 16], "bfloat16"),
+    "ones": ("sbuf", [128, 144], "bfloat16"),
+    "za": ("sbuf", [128, 144], "bfloat16"),
+    "zb": ("sbuf", [128, 144], "bfloat16"),
+    "ZP": ("sbuf", [128, 144], "bfloat16"),
+    "ZW": ("sbuf", [128, 144], "bfloat16"),
+    "ba": ("sbuf", [128, 128], "bfloat16"),
+    "BO": ("sbuf", [128, 128], "bfloat16"),
+    "tr": ("sbuf", [128, 128], "bfloat16"),
+    "TM": ("sbuf", [128, 128], "bfloat16"),
+    "ID": ("sbuf", [128, 128], "bfloat16"),
+    "NI": ("sbuf", [128, 128], "bfloat16"),
+    "HI": ("sbuf", [128, 128], "bfloat16"),
+    "mh": ("sbuf", [128, 192], "bfloat16"),
+    "pi": ("sbuf", [128, 1], "int32"),
+    "si": ("sbuf", [128, 1], "int32"),
+    "s0": ("sbuf", [128, 1], "float32"),
+    "s4": ("sbuf", [128, 1], "float32"),
+    "s613": ("sbuf", [128, 1], "float32"),
+    "sf": ("sbuf", [128, 1], "float32"),
+    "wti": ("sbuf", [128, 1], "int32"),
+    "thi": ("sbuf", [128, 1], "int32"),
+    "taui": ("sbuf", [128, 1], "int32"),
+    "wtf": ("sbuf", [128, 1], "float32"),
+    "thf": ("sbuf", [128, 1], "float32"),
+    "lim": ("sbuf", [128, 1], "float32"),
+    "ci": ("sbuf", [128, 1], "int32"),
+    "cj": ("sbuf", [128, 1], "int32"),
+    "hb": ("sbuf", [128, 4], "float32"),
+}
+for _t in range(RO):
+    SCRATCH["mail%d" % _t] = ("sbuf", [128, MW], "bfloat16")
+for _b in range(8):
+    SCRATCH["ps%d" % _b] = ("psum", [128, 512], "float32")
+
+SEMAPHORES = ["cV", "cS", "cP", "cG", "sent"] + ["arr%d" % t for t in range(RO)] + ["d%d" % i for i in range(40)]
+
+CYC = 0.00083 * 1.2
+GAT = 1.55
+FIX = {"V": 0.05, "S": 0.08, "P": 0.05, "G": 0.2, "Y": 0.1}
+WAKE = 0.1
+MAILT = 3.0
+VPEN = 0.0
+SLACK = 0.1
+
+
+def rank_program(g, core, T, topo):
+    rank = T.rank_of(core)
+    if rank is None:
+        return
+    AF, OP = ActivationFunctionType, AluOpType
+    V, SC, PE = g.vector, g.scalar, g.tensor
+    ps = [T["ps%d" % b] for b in range(8)]
+    tasks, lastw, readers = [], {}, {}
+
+    def add(eng, cost, emit, rd=(), wr=(), lat=0.0, sem=None, val=0, after=()):
+        i = len(tasks)
+        deps = set(after)
+        for k in rd:
+            if k in lastw:
+                deps.add(lastw[k])
+        for k in wr:
+            if k in lastw:
+                deps.add(lastw[k])
+            deps.update(readers.get(k, ()))
+        for k in wr:
+            lastw[k] = i
+            readers[k] = []
+        for k in rd:
+            if k not in wr:
+                readers.setdefault(k, []).append(i)
+        deps.discard(i)
+        k = (rd if eng == "P" else wr or ["out"])[-1]
+        lab = eng[0] + (k if isinstance(k, str) else k[0] + ("" if k[0] in ("mail", "A", "en") else str(k[-1])))
+        tasks.append(dict(eng=GE.get(lab, eng), cost=cost, emit=emit, deps=sorted(deps), lat=lat, sem=sem, val=val, lab=lab))
+        return i
+
+    nd = [0]
+
+    def dma(eng, out, in_, rd, wr, lat=2.5):
+        name = "d%d" % nd[0]
+        nd[0] += 1
+        q = {"Y": g.sync, "S": g.scalar}[eng]
+        add(eng, 0.06, lambda e: [q.dma_start(out, in_)], rd, wr, lat, name, 16)
+
+    def vec(cyc, emit, rd, wr):
+        add("V", max(64, cyc) * CYC + FIX["V"], lambda e: [emit()], rd, wr)
+
+    def act(cyc, emit, rd, wr):
+        add("S", cyc * CYC + FIX["S"], lambda e: [emit()], rd, wr)
+
+    def mm(cyc, emit, rd, wr):
+        add("P", cyc * CYC + FIX["P"], lambda e: emit(), rd, wr)
+
+    def gps(cost, emit, rd, wr):
+        add("G", cost, lambda e: [emit()], rd, wr)
+
+    dma("Y", T.wti[:], T.wt[:], [], ["wti"])
+    dma("Y", T.X[:, 1792:2048], T.x0[:, 1792:2048], [], ["Xs1"])
+    dma("Y", T.thi[:], T.th[:], [], ["thi"])
+    for q, (a, b) in enumerate(((0, 512), (512, 1024), (1024, 1536), (1536, 1792))):
+        dma("Y", T.X[:, a:b], T.x0[:, a:b], [], ["Xq%d" % q], 2.6 + 0.7 * q)
+    for j in range(8):
+        dma("Y", T.kdw[16 * j:16 * j + 16, :], T.kd[:], [], ["kd%d" % j], 4.0 + 0.6 * j)
+    dma("Y", T.taui[:], T.tau[:], [], ["taui"], 6.0)
+    vec(72, lambda: V.memset(T.ones[:], 1.0), [], ["ones"])
+    for q in range(4):
+        vec(1, lambda q=q: V.memset(T.hb[:, q:q + 1], H * (512 * q + 1 - N0)), [], ["hb%d" % q])
+    gps(1.0, lambda: g.iota(T.nam[:], [[1, 512]], 0, 0, allow_small_or_imprecise_dtypes=True), [], ["nam"])
+    for q in range(4):
+        act(512, lambda q=q: SC.activation(ps[q][:], T.nam[:], AF.Exp, bias=T.hb[:, q:q + 1], scale=H), ["hb%d" % q, "nam"], ["b%d" % q])
+    gps(0.15, lambda: g.iota(T.pi[:], [[1, 1]], 0, 1), [], ["pi"])
+    gps(0.15, lambda: g.iota(T.ki[:, 0:12], [[16 * 613, 12]], 0, 0), [], ["ki"])
+    gps(0.4, lambda: g.affine_select(T.za[:], T.ones[:], [[0, 9], [1, 16]], OP.is_equal, 0.0, -15, 0), ["ones"], ["za"])
+    gps(0.4, lambda: g.affine_select(T.zb[:], T.za[:], [[-16, 9], [0, 16]], OP.is_ge, 0.0, 0, 1), ["za"], ["zb"])
+    gps(0.4, lambda: g.affine_select(T.ZP[:], T.zb[:], [[16, 9], [0, 16]], OP.is_ge, 0.0, 15, -1), ["zb"], ["ZP"])
+    vec(1, lambda: V.tensor_copy(T.wtf[:], T.wti[:]), ["wti"], ["wtf"])
+    vec(72, lambda: V.tensor_scalar(T.ZW[:], T.ZP[:], T.wtf[:, 0:1], None, OP.mult), ["ZP", "wtf"], ["ZW"])
+    vec(1, lambda: V.tensor_scalar(T.si[:], T.pi[:], 15, None, OP.bitwise_and), ["pi"], ["si"])
+    vec(1, lambda: V.tensor_scalar(T.s613[:], T.si[:], 613.0, None, OP.mult), ["si"], ["s613"])
+    vec(12, lambda: V.tensor_scalar(T.kj[:, 0:12], T.ki[:, 0:12], T.s613[:, 0:1], None, OP.add), ["ki", "s613"], ["kj"])
+    vec(12, lambda: V.tensor_scalar(T.kl[:, 0:12], T.kj[:, 0:12], 2047, None, OP.bitwise_and), ["kj"], ["kl"])
+    vec(12, lambda: V.tensor_copy(T.k613[:, 0:12], T.kl[:, 0:12]), ["kl"], ["k613"])
+    vec(1, lambda: V.tensor_scalar(T.s0[:], T.si[:], 0.0, None, OP.is_equal), ["si"], ["s0"])
+    vec(1, lambda: V.tensor_copy(T.thf[:], T.thi[:]), ["thi"], ["thf"])
+
+    def kids(t):
+        B = S + t * G
+        b = B - G
+        src = ["Xs1"] if t == 0 else [("X", t - 1, k) for k in range(len(SG))]
+        n = 12
+
+        def um():
+            return [PE.matmul(ps[7][:, 256:256 + n], T.ZW[:, 15 - s:143 - s], T.X[:, b + s:b + NP:16], s == 0, s == 15) for s in range(16)]
+        mm(16 * 64, um, ["ZW"] + src, ["b7"])
+        vec(12, lambda: V.tensor_tensor(T.u1[:, 0:n], ps[7][:, 256:256 + n], T.k613[:, 0:n], OP.add), ["k613"], ["b7", "u1"])
+        vec(12, lambda: V.tensor_scalar(T.u2[:, 0:n], T.u1[:, 0:n], 2047, None, OP.bitwise_and), ["u1"], ["u2"])
+        vec(12, lambda: V.tensor_copy(T.UL[:, 0:n], T.u2[:, 0:n]), ["u2"], ["UL"])
+        vec(192 * GAT, lambda: V.tensor_scalar(T.e32[:], T.kdw[:, 0:2048].indirect(T.UL[:, 0:n]), B / 4096.0, -15.0 / 32, OP.mult, OP.add),
+            ["UL"] + ["kd%d" % j for j in range(8)], ["e32"])
+        vec(192, lambda: V.tensor_scalar(T.EL[:], T.e32[:], 2.0, T.s0[:, 0:1], OP.mult, OP.add), ["e32", "s0"], ["EL"])
+
+    kids(0)
+    for q, (a, b) in enumerate(((0, 512), (512, 1024), (1024, 1536), (1536, 2048))):
+        xk = ["Xq%d" % q] + (["Xs1"] if q == 3 else [])
+        vec(256, lambda a=a, b=b: V.tensor_scalar(T.f0s[:, a:b], T.X[:, a:b], T.thf[:, 0:1], -PLAIN, OP.is_lt, OP.mult), xk + ["thf"], ["f0s%d" % q])
+        act(512, lambda a=a, b=b: SC.activation(T.f1s[:, a:b], T.f0s[:, a:b], AF.Identity, bias=1.0, scale=2.0 ** WB / PLAIN), ["f0s%d" % q], ["f1s%d" % q])
+        vec(512, lambda a=a, b=b, q=q: V.tensor_tensor(T.W[:, 2 * a:2 * b:2], ps[q][:], T.f0s[:, a:b], OP.add), ["f0s%d" % q], ["b%d" % q, ("W0s", q)])
+        vec(512, lambda a=a, b=b, q=q: V.tensor_tensor(T.W[:, 2 * a + 1:2 * b:2], ps[q][:], T.f1s[:, a:b], OP.mult), ["f1s%d" % q], ["b%d" % q, ("W1s", q)])
+    vec(WIDE / 2, lambda: V.memset(T.rmax[:], FAR), [], ["rmax"])
+    vec(64, lambda: V.memset(T.rmax[:, 0:WIDE:16], -FAR), [], ["rmax"])
+    vec(WIDE / 2, lambda: V.memset(T.rmin[:], -FAR), [], ["rmin"])
+    vec(64, lambda: V.memset(T.rmin[:, 0:WIDE:16], FAR), [], ["rmin"])
+    gps(0.4, lambda: g.affine_select(T.ID[:], T.ones[:, 0:128], [[-1, 128]], OP.is_equal, 0.0, 0, 1), ["ones"], ["ID"])
+    vec(64, lambda: V.tensor_scalar(T.NI[:], T.ID[:], -1.0, None, OP.mult), ["ID"], ["NI"])
+    vec(64, lambda: V.tensor_scalar(T.HI[:], T.ID[:], 0.5, None, OP.mult), ["ID"], ["HI"])
+    vec(64, lambda: V.memset(T.mh[:], -0.5), [], ["mh"])
+    vec(1, lambda: V.tensor_copy(T.lim[:], T.taui[:]), ["taui"], ["lim"])
+    gps(0.4, lambda: g.affine_select(T.ba[:], T.ones[:, 0:128], [[-16, 8], [0, 16]], OP.is_ge, 0.0, 0, 1), ["ones"], ["ba"])
+    gps(0.4, lambda: g.affine_select(T.BO[:], T.ba[:], [[16, 8], [0, 16]], OP.is_ge, 0.0, 15, -1), ["ba"], ["BO"])
+    gps(0.4, lambda: g.affine_select(T.tr[:], T.BO[:], [[-1, 128]], OP.is_gt, 0.0, 0, 1), ["BO"], ["tr"])
+    vec(64, lambda: V.tensor_scalar(T.TM[:], T.tr[:], -1.0, None, OP.mult), ["tr"], ["TM"])
+    gps(0.15, lambda: g.iota(T.wi[:, 0:12], [[64, 12]], 192, 0, allow_small_or_imprecise_dtypes=True), [], ["wi"])
+    vec(1, lambda: V.tensor_scalar(T.s4[:], T.si[:], 4.0, None, OP.mult), ["si"], ["s4"])
+    vec(12, lambda: V.tensor_scalar(T.wc[:, 0:12], T.wi[:, 0:12], T.s4[:, 0:1], None, OP.add), ["wi", "s4"], ["wc"])
+    vec(12, lambda: V.memset(T.z12[:], 0.0), [], ["z12"])
+    gps(0.3, lambda: g.iota(T.mio[:], [[0, LASTN // 16], [1, 16]], 0, 0, allow_small_or_imprecise_dtypes=True), [], ["mio"])
+    vec(1, lambda: V.tensor_copy(T.sf[:], T.si[:]), ["si"], ["sf"])
+    vec(LASTN, lambda: V.tensor_scalar(T.msk[:], T.mio[:], T.sf[:, 0:1], None, OP.is_equal), ["mio", "sf"], ["msk"])
+    for t in range(RO):
+        gps(0.6, lambda t=t: g.iota(T.A[:, 256 * t:256 * t + 256], [[1, 256]], S + 256 * t, 0, allow_small_or_imprecise_dtypes=True), [], [("A", t)])
+        act(256, lambda t=t: SC.activation(T.en[:, 256 * t:256 * t + 256], T.A[:, 256 * t:256 * t + 256], AF.Exp, bias=T.hb[:, 0:1], scale=H), ["hb0", ("A", t)], [("en", t)])
+        if t < RO - 1:
+            act(CAP, lambda a=256 * t + NP: SC.activation(T.ng[:, a:a + CAP], T.en[:, a:a + CAP], AF.Copy, scale=-2.0 ** WB), [("en", t)], [("ngm", t)])
+        vec(32, lambda t=t: V.memset(T["mail%d" % t][:, 0:CAP], 0.0), [], [("mail", t)])
+    Wk = [("W%ds" % r, q) for r in range(2) for q in range(4)]
+    Xk = ["Xq0", "Xq1", "Xq2", "Xq3", "Xs1"]
+    for t in range(RO):
+        B = S + t * G
+        j0 = t * G
+        dfb = 0
+        for gi, grp in enumerate(SG):
+            db = 4 + gi % 2
+            for c in grp:
+                p0, n = CH[c]
+                a, z, w = 16 * p0, 16 * (p0 + n), 16 * n
+
+                def gat(e, a=a, z=z, p0=p0, n=n, B=B):
+                    src = T.W[:, 0:2 * B].indirect(T.EL[:, p0:p0 + n])
+                    if e == "V":
+                        return [V.tensor_copy(T.gk[:, a:z], src)]
+                    return [SC.activation(T.gk[:, a:z], src, AF.Copy)]
+                add("VS", w * GAT * CYC + 0.06, gat, ["EL"] + Wk, [("gk", c)])
+                act(w, lambda a=a, z=z: SC.activation(T.ga[:, a:z], T.gk[:, a:z], AF.Abs), [("gk", c)], [("ga", c)])
+                vec(w / 2, lambda a=a, z=z, w=w: V.tensor_tensor_scan(T.sM[:, a:z], T.rmax[:, 0:w], T.gk[:, a:z], 0.0, OP.min, OP.max), ["rmax", ("gk", c)], [("sM", c)])
+                vec(n / 2, lambda a=a, z=z, p0=p0, n=n: V.tensor_scalar(T.nrm[:, p0:p0 + n], T.sM[:, a + 15:z:16], 0.0, 2.0 ** -WB, OP.is_ge, OP.max), [("sM", c)], [("nrm", c)])
+                vec(w / 2, lambda a=a, z=z, w=w: V.tensor_tensor_scan(T.sm[:, a:z], T.rmin[:, 0:w], T.ga[:, a:z], 0.0, OP.max, OP.min), ["rmin", ("ga", c)], [("sm", c)])
+                l0, l1, l2 = 2 * p0, 2 * p0 + n, 2 * (p0 + n)
+                vec(2 * n, lambda a=a, z=z, p0=p0, n=n: V.tensor_tensor(T.loc[:, p0:p0 + n], T.sm[:, a + 15:z:16], T.nrm[:, p0:p0 + n], OP.mult), [("sm", c), ("nrm", c)], [("loc", c)])
+                vec(2 * n, lambda a=a, z=z, p0=p0, n=n: V.tensor_tensor(T.hic[:, p0:p0 + n], T.sM[:, a + 15:z:16], T.loc[:, p0:p0 + n], OP.max), [("sM", c), ("loc", c)], [("hic", c)])
+                for nm, cd, q0, q1 in (("xl", "loc", l0, l1), ("xh", "hic", l1, l2)):
+                    act(n, lambda cd=cd, q0=q0, q1=q1, p0=p0, n=n: SC.activation(T.lh[:, q0:q1], T[cd][:, p0:p0 + n], AF.Ln), [(cd, c)], [("lh", nm, c)])
+                vec(2 * n, lambda l0=l0, l2=l2: V.tensor_scalar(T.LH[:, l0:l2], T.lh[:, l0:l2], 1.0 / H, N0 - 1 + 0.245, OP.mult, OP.add), [("lh", "xl", c), ("lh", "xh", c)], [("LH", c)])
+                for nm, q0, q1 in (("xh", l1, l2), ("xl", l0, l1)):
+                    def gx(e, nm=nm, q0=q0, q1=q1, a=a, z=z, B=B):
+                        src = T.X[:, 0:B].indirect(T.LH[:, q0:q1])
+                        if e == "V":
+                            return [V.tensor_copy(T[nm][:, a:z], src)]
+                        return [SC.activation(T[nm][:, a:z], src, AF.Copy)]
+                    add("VS", w * GAT * CYC + 0.06, gx, [("LH", c)] + Xk, [(nm, c)])
+                dk = []
+                for s in range(a, z, 512):
+                    e_ = min(s + 512, z)
+                    if (c, (s - a) // 512) in DV:
+                        vec(2 * (e_ - s), lambda s=s, e_=e_: V.tensor_tensor(T.df[:, s:e_], T.xl[:, s:e_], T.xh[:, s:e_], OP.subtract), [("xl", c), ("xh", c)], [("df", s)])
+                        act(e_ - s, lambda s=s, e_=e_: SC.activation(T.da[:, s:e_], T.df[:, s:e_], AF.Abs), [("df", s)], [("da", s)])
+                        dk.append(("da", s))
+                        continue
+                    bk = dfb % 4
+                    dfb += 1
+                    mm(e_ - s, lambda s=s, e_=e_, bk=bk: [PE.matmul(ps[bk][:, 0:e_ - s], T.NI[:], T.xh[:, s:e_], True, False)], ["NI", ("xh", c)], ["b%d" % bk])
+                    mm(e_ - s, lambda s=s, e_=e_, bk=bk: [PE.matmul(ps[bk][:, 0:e_ - s], T.ID[:], T.xl[:, s:e_], False, True)], ["ID", ("xl", c)], ["b%d" % bk])
+                    act(e_ - s, lambda s=s, e_=e_, bk=bk: SC.activation(T.da[:, s:e_], ps[bk][:, 0:e_ - s], AF.Abs), [], ["b%d" % bk, ("da", s)])
+                    dk.append(("da", s))
+
+                def dm(a=a, z=z, p0=p0, n=n, db=db):
+                    return [PE.matmul(ps[db][:, p0:p0 + n], T.ZP[:, 15 - p:143 - p], T.da[:, a + p:z:16], p == 0, p == 15) for p in range(16)]
+                mm(16 * max(64, n), dm, ["ZP"] + dk, ["b%d" % db])
+                vec(w / 2, lambda a=a, z=z, w=w: V.tensor_tensor_scan(T.sl[:, a:z], T.rmax[:, 0:w], T.xl[:, a:z], 0.0, OP.min, OP.max), ["rmax", ("xl", c)], [("sl", c)])
+                vec(w / 2, lambda a=a, z=z, w=w: V.tensor_tensor_scan(T.sh[:, a:z], T.rmin[:, 0:w], T.xh[:, a:z], 0.0, OP.max, OP.min), ["rmin", ("xh", c)], [("sh", c)])
+            p0 = CH[grp[0]][0]
+            n = sum(CH[c][1] for c in grp)
+            a, z = 16 * p0, 16 * (p0 + n)
+            vec(n, lambda p0=p0, n=n, db=db: V.tensor_scalar(T.far[:, p0:p0 + n], ps[db][:, p0:p0 + n], T.lim[:, 0:1], None, OP.is_gt), ["lim"], ["b%d" % db, ("far", gi)])
+
+            def xm(a=a, z=z, n=n):
+                o = ps[7][:, 0:n]
+                return [PE.matmul(o, T.HI[:], T.mh[:, 0:n], True, False),
+                        PE.matmul(o, T.HI[:], T.sl[:, a + 15:z:16], False, False),
+                        PE.matmul(o, T.HI[:], T.sh[:, a + 15:z:16], False, True)]
+            mm(3 * max(64, n), xm, ["HI", "mh"] + [(k, c) for c in grp for k in ("sl", "sh")], ["b7"])
+            vec(n, lambda p0=p0, n=n, B=B: V.tensor_scalar(T.X[:, B + p0:B + p0 + n], ps[7][:, 0:n], MAGIC, MAGIC, OP.add, OP.subtract), [], ["b7", ("X", t, gi)])
+            m, c0 = n // 16, p0 // 16
+            last = gi == len(SG) - 1
+            if last:
+                mm(n, lambda p0=p0, n=n: [PE.matmul(ps[6][:, 128:128 + n], T.BO[:], T.far[:, p0:p0 + n], True, True)], ["BO", ("far", gi)], ["b6"])
+                vec(n, lambda n=n: V.tensor_tensor(T.cm[:], ps[6][:, 128:128 + n], T.msk[:], OP.mult), ["msk"], ["b6", "cm"])
+                vec(n / 2, lambda n=n: V.tensor_tensor_scan(T.cs[:], T.rmax[:, 0:n], T.cm[:], 0.0, OP.min, OP.max), ["rmax", "cm"], ["cs"])
+                vec(m, lambda c0=c0, m=m, n=n: V.tensor_scalar(T.Fb[:, c0:c0 + m], T.cs[:, 15:n:16], 1.0, None, OP.is_ge), ["cs"], [("Fb", gi)])
+            else:
+                def cm(p0=p0, n=n, m=m):
+                    return [PE.matmul(ps[6][:, 0:m], T.ZP[:, 15 - s:143 - s], T.far[:, p0 + s:p0 + n:16], s == 0, s == 15) for s in range(16)]
+                mm(16 * 64, cm, ["ZP", ("far", gi)], ["b6"])
+                vec(m, lambda c0=c0, m=m: V.tensor_scalar(T.Fb[:, c0:c0 + m], ps[6][:, 0:m], 1.0, None, OP.is_ge), [], ["b6", ("Fb", gi)])
+            vec(m, lambda c0=c0, m=m: V.tensor_tensor_scan(T.inc[:, c0:c0 + m], T.Fb[:, c0:c0 + m], T.z12[:, 0:m], T.inc[:, c0 - 1:c0] if c0 else 0.0, OP.add, OP.max),
+                ["z12", ("Fb", gi)] + ([("inc", gi - 1)] if c0 else []), [("inc", gi)])
+            vec(2 * m, lambda c0=c0, m=m: V.tensor_tensor(T.Fw[:, c0:c0 + m], T.Fb[:, c0:c0 + m], T.wc[:, c0:c0 + m], OP.mult), ["wc", ("Fb", gi)], [("Fw", gi)])
+
+            def cu(c0=c0, m=m):
+                o = ps[6][:, 32:32 + m]
+                return [PE.matmul(o, T.ID[:], T.wc[:, c0:c0 + m], True, False),
+                        PE.matmul(o, T.TM[:], T.Fb[:, c0:c0 + m], False, False),
+                        PE.matmul(o, T.BO[:], T.inc[:, c0:c0 + m], False, False),
+                        PE.matmul(o, T.NI[:], T.Fw[:, c0:c0 + m], False, True)]
+            mm(4 * 64, cu, ["ID", "TM", "BO", "NI", "wc", ("Fb", gi), ("inc", gi), ("Fw", gi)], ["b6"])
+            vec(m, lambda c0=c0, m=m: V.tensor_scalar(T.slots[:, c0:c0 + m], ps[6][:, 32:32 + m], -1.0, None, OP.add), [], ["b6", ("slots", gi)])
+            vec(3.5 * n, lambda c0=c0, m=m, p0=p0, n=n, B=B, t=t: V.tensor_copy(T["mail%d" % t][:, 0:MW].indirect(T.slots[:, c0:c0 + m]), T.X[:, B + p0:B + p0 + n]),
+                [("slots", gi), ("X", t, gi)], [("mail", t)])
+        dst = T.cores[(rank + 1 + t % (len(T.cores) - 1)) % len(T.cores)]
+        eng = topo.engines(core, dst)[:8]
+        msk = sum(1 << e for e in eng)
+        rid, pid = topo.addr(dst)[:2]
+        ne = len(eng)
+        m0, m1 = B + NP, B + G
+        snd = add("G", 1.0, lambda e, t=t, m0=m0, m1=m1, rid=rid, pid=pid, msk=msk: [g.remote_dma(T.X[:, m0:m1], T["mail%d" % t][:, 0:CAP], T.sem["arr%d" % t], T.sem.sent, pid, rid, msk)],
+                  [("mail", t)], [], sem="sent", val=ne)
+        add("R", 0.0, None, [], [("X", t, "m")], lat=MAILT, sem="arr%d" % t, val=ne, after=[snd])
+        nl = [("loc", c) for c in range(NCH)]
+        nf = [("far", k) for k in range(len(SG))]
+        nx = [("X", t, k) for k in range(len(SG))]
+        vec(2 * NP, lambda j0=j0: V.tensor_tensor(T.fn[:], T.far[:], T.en[:, j0:j0 + NP], OP.mult), nf + [("en", t)], ["fn"])
+        vec(2 * NP, lambda j0=j0: V.tensor_tensor(T.en[:, j0:j0 + NP], T.loc[:], T.fn[:], OP.max), nl + ["fn"], [("en", t)])
+        act(NP, lambda j0=j0: SC.activation(T.ln1[:], T.en[:, j0:j0 + NP], AF.Ln), [("en", t)], ["ln1"])
+        act(NP, lambda: SC.activation(T.ln2[:], T.ln1[:], AF.Identity, bias=MAGIC + N0 - 1, scale=1.0 / H), ["ln1"], ["ln2"])
+        act(NP, lambda j0=j0: SC.activation(T.A[:, j0:j0 + NP], T.ln2[:], AF.Identity, bias=-MAGIC), ["ln2"], [("A", t)])
+        if t < RO - 1:
+            kids(t + 1)
+            for lab, q0, q1, rd in (("p", 0, NP, nx), ("m", NP, G, [("X", t, "m")])):
+                vec((q1 - q0) / 2, lambda B=B, q0=q0, q1=q1: V.tensor_scalar(T.f0[:, q0:q1], T.X[:, B + q0:B + q1], T.thf[:, 0:1], -PLAIN, OP.is_lt, OP.mult), rd + ["thf"], ["f0" + lab])
+                if lab == "p":
+                    act(NP, lambda j0=j0: SC.activation(T.ng[:, j0:j0 + NP], T.en[:, j0:j0 + NP], AF.Copy, scale=-2.0 ** WB), [("en", t)], [("ngp", t)])
+                w0, w1, wz = 2 * (B + q0), 2 * (B + q0) + 1, 2 * (B + q1)
+                vec(2 * (q1 - q0), lambda q0=q0, q1=q1, w0=w0, wz=wz, j0=j0: V.tensor_tensor(T.W[:, w0:wz:2], T.en[:, j0 + q0:j0 + q1], T.f0[:, q0:q1], OP.add),
+                    [("en", t), "f0" + lab], [("W", t, "0" + lab)])
+                vec(2 * (q1 - q0), lambda q0=q0, q1=q1, w0=w0, w1=w1, wz=wz, j0=j0: V.tensor_tensor(T.W[:, w1:wz:2], T.ng[:, j0 + q0:j0 + q1], T.W[:, w0:wz:2], OP.max),
+                    [("ng" + lab, t), ("W", t, "0" + lab)], [("W", t, "1" + lab)])
+                Wk += [("W", t, "0" + lab), ("W", t, "1" + lab)]
+            Xk += nx + [("X", t, "m")]
+            mm(64, lambda: [PE.matmul(ps[6][:, 64:65], T.ones[:, 0:128], T.inc[:, 11:12], True, True)], ["ones", ("inc", len(SG) - 1)], ["b6"])
+            vec(1, lambda: V.tensor_copy(T.ci[:], ps[6][:, 64:65]), [], ["b6", "ci"])
+            vec(1, lambda: V.tensor_scalar(T.cj[:], T.ci[:], 15, None, OP.bitwise_and), ["ci"], ["cj"])
+            vec(1, lambda: V.tensor_tensor(T.lim[:], T.taui[:], T.cj[:], OP.add), ["cj", "taui"], ["lim"])
+        dma("Y", T.yx[:, j0:j0 + NP], T.X[:, B:B + NP], nx, [])
+        dma("Y", T.ya[:, j0:j0 + G], T.A[:, j0:j0 + G], [("A", t)], [])
+        dma("Y", T.yx[:, j0 + NP:j0 + G], T.X[:, B + NP:B + G], [("X", t, "m")], [])
+    emit_all(g, T, tasks)
+
+
+def plan(tasks):
+    nt = len(tasks)
+    succ = [[] for _ in range(nt)]
+    for i, k in enumerate(tasks):
+        for d in k["deps"]:
+            succ[d].append(i)
+    prio = [0.0] * nt
+    for i in range(nt - 1, -1, -1):
+        prio[i] = tasks[i]["cost"] + tasks[i]["lat"] + max([prio[s] + WAKE for s in succ[i]], default=0.0)
+    left = [len(k["deps"]) for k in tasks]
+    ready = [0.0] * nt
+    free = {"V": 0.0, "S": 0.0, "P": 0.0, "G": 0.0, "Y": 0.0, "R": 0.0}
+    avail = {i for i in range(nt) if left[i] == 0}
+    where, seq = [None] * nt, []
+    for i in range(nt):
+        prio[i] += PRI.get(tasks[i]["lab"], 0.0)
+    while avail:
+        cand = []
+        for i in avail:
+            for q in tasks[i]["eng"]:
+                st = ready[i] if q == "R" else max(free[q], ready[i])
+                cand.append((st + (VPEN if q == "V" and tasks[i]["eng"] == "VS" else 0.0), -prio[i], i, q, st))
+        first = min(cand)
+        _, i, q, st = min(x[1:] for x in cand if x[3] == first[3] and x[0] <= first[0] + SLACK)
+        avail.discard(i)
+        k = tasks[i]
+        end = st + k["cost"]
+        if q != "R":
+            free[q] = end
+        where[i] = q
+        seq.append(i)
+        for s in succ[i]:
+            ready[s] = max(ready[s], end + k["lat"] + WAKE)
+            left[s] -= 1
+            if left[s] == 0:
+                avail.add(s)
+    return where, seq, max(free.values())
+
+
+def emit_all(g, T, tasks):
+    where, seq, _ = plan(tasks)
+    nt = len(tasks)
+    at = [0] * nt
+    for n, i in enumerate(seq):
+        at[i] = n
+    queues = {"V": g.vector, "S": g.scalar, "P": g.tensor, "G": g, "Y": g.sync}
+    count = {}
+    seen = {q: {} for q in queues}
+    own = [None] * nt
+    clock = [None] * nt
+    for i in seq:
+        k, q = tasks[i], where[i]
+        if q == "R":
+            own[i] = (k["sem"], k["val"])
+            clock[i] = {k["sem"]: k["val"]}
+            count[k["sem"]] = k["val"]
+            continue
+        for d in sorted(k["deps"], key=lambda d: -at[d]):
+            s, v = own[d]
+            if seen[q].get(s, 0) < v:
+                queues[q].wait_ge(T.sem[s], v)
+                for s2, v2 in clock[d].items():
+                    seen[q][s2] = max(seen[q].get(s2, 0), v2)
+        out = k["emit"](q)
+        s = k["sem"] or "c" + q
+        n = k["val"] if k["sem"] else 1
+        for ins in out:
+            if s != "sent":
+                ins.then_inc(T.sem[s], n)
+            count[s] = count.get(s, 0) + n
+        own[i] = (s, count[s])
+        clock[i] = dict(seen[q])
+        clock[i][s] = count[s]
+    for s in sorted(count):
+        if seen["G"].get(s, 0) < count[s]:
+            g.wait_ge(T.sem[s], count[s])

@@ -4,117 +4,77 @@ from concourse.mybir import dt, AluOpType, AxisListType, ActivationFunctionType
 S, NP, CAP, RO, G = 2048, 192, 64, 5, 256
 TOT = S + RO * G
 CH = [(0, 64), (64, 64), (128, 64)]
-SG = [[0, 1, 2]]
-GE = {"Vxh1": "S", "Vxl2": "S", "Vgk2": "S", "Vxl0": "S"}
-PRI = {"Vf0p": 3, "Vf0s2": 12, "Vs0": 12, "Vsf": 6, "Slh0": 1.5, "VTM": 6, "Sga1": 12, "Vnrm0": -1.5, "Ve32": -1.5, "Vf0s1": -1.5,
-       "VW1s0": 1.5, "VsM1": -3, "VsM0": -6, "VZW": -1.5, "Vs613": 12}
+GE = {"Vgk0": "V", "Vgk2": "V", "Vxh0": "V", "Vxh1": "S", "Vxl0": "S", "Vxl1": "V", "Vxl2": "S"}
+PRI = {"Sc0": 6, "Vfn": -3, "Vsh2": -6, "VUL": -12, "Vxl0": -12, "Sda2048": 6, "Sda2560": 3, "VW1s1": -12, "Sda0": 12, "Vkl": -6,
+       "Vwc": -1.5, "VW1s0": -3, "Vtauf": -3, "Vmsk": -3, "VZW": -3, "Sen": 20}
 DV = [(2, 1)]
 NCH = len(CH)
 WIDE = 16 * max(n for _, n in CH)
-LASTN = sum(CH[c][1] for c in SG[-1])
-N0 = 2590
-H = 63 * math.log(2.0) / N0
-WB = 81
+N0 = 3336
+WB = 63
+H = WB * math.log(2.0) / N0
 PLAIN = 2.0 ** 99
 FAR = 9.0e29
 MW = 1152
-MAGIC = 8388608.0
+MAGIC = 12582912.0
 
 SCRATCH = {
-    "X": ("sbuf", [128, TOT], "bfloat16"),
+    "X": ("sbuf", [128, N0 + TOT], "bfloat16"),
     "W": ("sbuf", [128, 2 * TOT], "bfloat16"),
     "kdw": ("sbuf", [128, 2048], "int32"),
     "nam": ("sbuf", [128, 512], "float32"),
     "A": ("sbuf", [128, RO * G], "float32"),
     "en": ("sbuf", [128, RO * G], "bfloat16"),
-    "f0s": ("sbuf", [128, 2048], "bfloat16"),
-    "f1s": ("sbuf", [128, 2048], "bfloat16"),
-    "f0": ("sbuf", [128, 256], "bfloat16"),
     "ng": ("sbuf", [128, RO * G], "bfloat16"),
-    "gk": ("sbuf", [128, 3072], "bfloat16"),
-    "ga": ("sbuf", [128, 3072], "bfloat16"),
-    "sM": ("sbuf", [128, 3072], "bfloat16"),
-    "sm": ("sbuf", [128, 3072], "bfloat16"),
-    "xl": ("sbuf", [128, 3072], "bfloat16"),
-    "xh": ("sbuf", [128, 3072], "bfloat16"),
-    "sl": ("sbuf", [128, 3072], "bfloat16"),
-    "sh": ("sbuf", [128, 3072], "bfloat16"),
-    "df": ("sbuf", [128, 3072], "bfloat16"),
-    "da": ("sbuf", [128, 3072], "bfloat16"),
-    "rmax": ("sbuf", [128, WIDE], "bfloat16"),
-    "rmin": ("sbuf", [128, WIDE], "bfloat16"),
-    "nrm": ("sbuf", [128, 192], "bfloat16"),
-    "loc": ("sbuf", [128, 192], "bfloat16"),
-    "hic": ("sbuf", [128, 192], "bfloat16"),
+    "es": ("sbuf", [128, 2048], "bfloat16"),
+    "ns": ("sbuf", [128, 2048], "bfloat16"),
+    "f0s": ("sbuf", [128, 2048], "bfloat16"),
+    "f0": ("sbuf", [128, 256], "bfloat16"),
+    "kb": ("sbuf", [128, 1], "float32"),
+    "UL": ("sbuf", [128, 16], "uint16"),
+    "EL": ("sbuf", [128, 192], "uint16"),
     "lh": ("sbuf", [128, 384], "float32"),
     "LH": ("sbuf", [128, 384], "uint16"),
     "ln1": ("sbuf", [128, 192], "float32"),
     "ln2": ("sbuf", [128, 192], "float32"),
-    "EL": ("sbuf", [128, 192], "uint16"),
-    "e32": ("sbuf", [128, 192], "int32"),
-    "far": ("sbuf", [128, 192], "bfloat16"),
-    "fn": ("sbuf", [128, 192], "bfloat16"),
-    "cm": ("sbuf", [128, LASTN], "bfloat16"),
-    "cs": ("sbuf", [128, LASTN], "bfloat16"),
-    "msk": ("sbuf", [128, LASTN], "bfloat16"),
-    "mio": ("sbuf", [128, LASTN], "float32"),
-    "UL": ("sbuf", [128, 16], "uint16"),
-    "u1": ("sbuf", [128, 16], "int32"),
-    "u2": ("sbuf", [128, 16], "int32"),
-    "k613": ("sbuf", [128, 16], "float32"),
-    "ki": ("sbuf", [128, 16], "int32"),
-    "kj": ("sbuf", [128, 16], "int32"),
-    "kl": ("sbuf", [128, 16], "int32"),
-    "wi": ("sbuf", [128, 16], "float32"),
-    "wc": ("sbuf", [128, 16], "bfloat16"),
-    "Fb": ("sbuf", [128, 16], "bfloat16"),
-    "inc": ("sbuf", [128, 16], "bfloat16"),
-    "Fw": ("sbuf", [128, 16], "bfloat16"),
-    "slots": ("sbuf", [128, 16], "uint16"),
-    "z12": ("sbuf", [128, 16], "bfloat16"),
-    "ones": ("sbuf", [128, 144], "bfloat16"),
-    "za": ("sbuf", [128, 144], "bfloat16"),
-    "zb": ("sbuf", [128, 144], "bfloat16"),
     "ZP": ("sbuf", [128, 144], "bfloat16"),
-    "ZW": ("sbuf", [128, 144], "bfloat16"),
-    "ba": ("sbuf", [128, 128], "bfloat16"),
-    "BO": ("sbuf", [128, 128], "bfloat16"),
-    "tr": ("sbuf", [128, 128], "bfloat16"),
-    "TM": ("sbuf", [128, 128], "bfloat16"),
-    "ID": ("sbuf", [128, 128], "bfloat16"),
-    "NI": ("sbuf", [128, 128], "bfloat16"),
-    "HI": ("sbuf", [128, 128], "bfloat16"),
-    "mh": ("sbuf", [128, 192], "bfloat16"),
-    "pi": ("sbuf", [128, 1], "int32"),
-    "si": ("sbuf", [128, 1], "int32"),
-    "s0": ("sbuf", [128, 1], "float32"),
-    "s4": ("sbuf", [128, 1], "float32"),
-    "s613": ("sbuf", [128, 1], "float32"),
-    "sf": ("sbuf", [128, 1], "float32"),
-    "wti": ("sbuf", [128, 1], "int32"),
-    "thi": ("sbuf", [128, 1], "int32"),
-    "taui": ("sbuf", [128, 1], "int32"),
-    "wtf": ("sbuf", [128, 1], "float32"),
-    "thf": ("sbuf", [128, 1], "float32"),
-    "lim": ("sbuf", [128, 1], "float32"),
-    "ci": ("sbuf", [128, 1], "int32"),
-    "cj": ("sbuf", [128, 1], "int32"),
-    "hb": ("sbuf", [128, 4], "float32"),
+    "slots": ("sbuf", [128, 16], "uint16"),
 }
+for _k in ("gk", "ga", "sM", "sm", "xl", "xh", "sl", "sh", "df", "da"):
+    SCRATCH[_k] = ("sbuf", [128, 16 * NP], "bfloat16")
+for _k in ("nrm", "c0", "loc", "hic", "far", "fn", "cm", "cs", "msk", "mh"):
+    SCRATCH[_k] = ("sbuf", [128, NP], "bfloat16")
+for _k in ("rmax", "rmin"):
+    SCRATCH[_k] = ("sbuf", [128, WIDE], "bfloat16")
+for _k in ("ones", "za", "zb", "ZW"):
+    SCRATCH[_k] = ("sbuf", [128, 144], "bfloat16")
+for _k in ("ba", "BO", "tr", "TM", "ID", "NI", "HI", "o16"):
+    SCRATCH[_k] = ("sbuf", [128, 128], "bfloat16")
+for _k in ("wc", "inc", "Fw", "z12", "q15"):
+    SCRATCH[_k] = ("sbuf", [128, 16], "bfloat16")
+for _k in ("u1", "u2", "ki", "kj", "kl"):
+    SCRATCH[_k] = ("sbuf", [128, 16], "int32")
+for _k in ("k613", "wi"):
+    SCRATCH[_k] = ("sbuf", [128, 16], "float32")
+SCRATCH["mio"] = ("sbuf", [128, NP], "float32")
+for _k in ("pi", "si", "wti", "thi", "taui"):
+    SCRATCH[_k] = ("sbuf", [128, 1], "int32")
+for _k in ("s0", "s4", "s613", "sf", "wtf", "thf", "tauf", "lim", "cf", "cg", "tc"):
+    SCRATCH[_k] = ("sbuf", [128, 1], "float32")
 for _t in range(RO):
+    SCRATCH["min%d" % _t] = ("sbuf", [128, CAP], "bfloat16")
     SCRATCH["mail%d" % _t] = ("sbuf", [128, MW], "bfloat16")
 for _b in range(8):
     SCRATCH["ps%d" % _b] = ("psum", [128, 512], "float32")
 
 SEMAPHORES = ["cV", "cS", "cP", "cG", "sent"] + ["arr%d" % t for t in range(RO)] + ["d%d" % i for i in range(40)]
 
-CYC = 0.00083 * 1.2
-GAT = 1.55
-FIX = {"V": 0.05, "S": 0.08, "P": 0.05, "G": 0.2, "Y": 0.1}
-WAKE = 0.1
-MAILT = 3.0
-VPEN = 0.0
-SLACK = 0.1
+CYC = 0.00083 * 1.05
+GAT = 1.4
+FIX = {"V": 0.04, "S": 0.07, "P": 0.03, "G": 0.2, "Y": 0.1}
+WAKE = 0.08
+MAILT = 2.0
+SLACK = 0.2
 
 
 def rank_program(g, core, T, topo):
@@ -150,39 +110,45 @@ def rank_program(g, core, T, topo):
 
     nd = [0]
 
-    def dma(eng, out, in_, rd, wr, lat=2.5):
+    def dma(out, in_, rd, wr, lat=2.5):
         name = "d%d" % nd[0]
         nd[0] += 1
-        q = {"Y": g.sync, "S": g.scalar}[eng]
-        add(eng, 0.06, lambda e: [q.dma_start(out, in_)], rd, wr, lat, name, 16)
+        add("Y", 0.06, lambda e: [g.sync.dma_start(out, in_)], rd, wr, lat, name, 16)
 
     def vec(cyc, emit, rd, wr):
         add("V", max(64, cyc) * CYC + FIX["V"], lambda e: [emit()], rd, wr)
 
-    def act(cyc, emit, rd, wr):
-        add("S", cyc * CYC + FIX["S"], lambda e: [emit()], rd, wr)
+    def act(cyc, emit, rd, wr, after=()):
+        add("S", cyc * CYC + FIX["S"], lambda e: [emit()], rd, wr, after=after)
 
     def mm(cyc, emit, rd, wr):
         add("P", cyc * CYC + FIX["P"], lambda e: emit(), rd, wr)
 
-    def gps(cost, emit, rd, wr):
-        add("G", cost, lambda e: [emit()], rd, wr)
+    def gps(cost, emit, rd, wr, after=()):
+        add("G", cost, lambda e: [emit()], rd, wr, after=after)
 
-    dma("Y", T.wti[:], T.wt[:], [], ["wti"])
-    dma("Y", T.X[:, 1792:2048], T.x0[:, 1792:2048], [], ["Xs1"])
-    dma("Y", T.thi[:], T.th[:], [], ["thi"])
+    dma(T.wti[:], T.wt[:], [], ["wti"])
+    dma(T.X[:, 1792:2048], T.x0[:, 1792:2048], [], ["Xs1"])
+    dma(T.thi[:], T.th[:], [], ["thi"])
     for q, (a, b) in enumerate(((0, 512), (512, 1024), (1024, 1536), (1536, 1792))):
-        dma("Y", T.X[:, a:b], T.x0[:, a:b], [], ["Xq%d" % q], 2.6 + 0.7 * q)
+        dma(T.X[:, a:b], T.x0[:, a:b], [], ["Xq%d" % q], 2.6 + 0.7 * q)
     for j in range(8):
-        dma("Y", T.kdw[16 * j:16 * j + 16, :], T.kd[:], [], ["kd%d" % j], 4.0 + 0.6 * j)
-    dma("Y", T.taui[:], T.tau[:], [], ["taui"], 6.0)
+        dma(T.kdw[16 * j:16 * j + 16, :], T.kd[:], [], ["kd%d" % j], 4.0 + 0.6 * j)
+    dma(T.taui[:], T.tau[:], [], ["taui"], 6.0)
+    dma(T.X[:, N0:N0 + S], T.x0[:], [], ["Xd"], 9.0)
     vec(72, lambda: V.memset(T.ones[:], 1.0), [], ["ones"])
-    for q in range(4):
-        vec(1, lambda q=q: V.memset(T.hb[:, q:q + 1], H * (512 * q + 1 - N0)), [], ["hb%d" % q])
     gps(1.0, lambda: g.iota(T.nam[:], [[1, 512]], 0, 0, allow_small_or_imprecise_dtypes=True), [], ["nam"])
+    gps(0.4, lambda: g.affine_select(T.ID[:], T.ones[:, 0:128], [[-1, 128]], OP.is_equal, 0.0, 0, 1), ["ones"], ["ID"])
     for q in range(4):
-        act(512, lambda q=q: SC.activation(ps[q][:], T.nam[:], AF.Exp, bias=T.hb[:, q:q + 1], scale=H), ["hb%d" % q, "nam"], ["b%d" % q])
+        a, b = 512 * q, 512 * q + 512
+        act(512, lambda a=a, b=b: SC.activation(T.es[:, a:b], T.nam[:], AF.Exp, bias=H * (a + 1 - N0), scale=H), ["nam"], ["es%d" % q])
+    for q in range(4):
+        a, b = 512 * q, 512 * q + 512
+        act(512, lambda a=a, b=b: SC.activation(T.ns[:, a:b], T.es[:, a:b], AF.Copy, scale=-2.0 ** WB), ["es%d" % q], ["ns%d" % q])
     gps(0.15, lambda: g.iota(T.pi[:], [[1, 1]], 0, 1), [], ["pi"])
+
+    def fill(out, n, value, key):
+        act(n, lambda: SC.activation(out, T.nam[:, 0:n], AF.Identity, bias=value, scale=0.0), ["nam"], [key])
     gps(0.15, lambda: g.iota(T.ki[:, 0:12], [[16 * 613, 12]], 0, 0), [], ["ki"])
     gps(0.4, lambda: g.affine_select(T.za[:], T.ones[:], [[0, 9], [1, 16]], OP.is_equal, 0.0, -15, 0), ["ones"], ["za"])
     gps(0.4, lambda: g.affine_select(T.zb[:], T.za[:], [[-16, 9], [0, 16]], OP.is_ge, 0.0, 0, 1), ["za"], ["zb"])
@@ -194,13 +160,14 @@ def rank_program(g, core, T, topo):
     vec(12, lambda: V.tensor_scalar(T.kj[:, 0:12], T.ki[:, 0:12], T.s613[:, 0:1], None, OP.add), ["ki", "s613"], ["kj"])
     vec(12, lambda: V.tensor_scalar(T.kl[:, 0:12], T.kj[:, 0:12], 2047, None, OP.bitwise_and), ["kj"], ["kl"])
     vec(12, lambda: V.tensor_copy(T.k613[:, 0:12], T.kl[:, 0:12]), ["kl"], ["k613"])
-    vec(1, lambda: V.tensor_scalar(T.s0[:], T.si[:], 0.0, None, OP.is_equal), ["si"], ["s0"])
+    vec(1, lambda: V.tensor_scalar(T.s0[:], T.si[:], 0.0, float(TOT), OP.is_equal, OP.mult), ["si"], ["s0"])
+    vec(1, lambda: V.tensor_scalar(T.kb[:], T.s0[:], 15.0 / 32, None, OP.subtract), ["s0"], ["kb"])
     vec(1, lambda: V.tensor_copy(T.thf[:], T.thi[:]), ["thi"], ["thf"])
 
     def kids(t):
         B = S + t * G
         b = B - G
-        src = ["Xs1"] if t == 0 else [("X", t - 1, k) for k in range(len(SG))]
+        src = ["Xs1"] if t == 0 else [("X", t - 1, 0)]
         n = 12
 
         def um():
@@ -209,173 +176,190 @@ def rank_program(g, core, T, topo):
         vec(12, lambda: V.tensor_tensor(T.u1[:, 0:n], ps[7][:, 256:256 + n], T.k613[:, 0:n], OP.add), ["k613"], ["b7", "u1"])
         vec(12, lambda: V.tensor_scalar(T.u2[:, 0:n], T.u1[:, 0:n], 2047, None, OP.bitwise_and), ["u1"], ["u2"])
         vec(12, lambda: V.tensor_copy(T.UL[:, 0:n], T.u2[:, 0:n]), ["u2"], ["UL"])
-        vec(192 * GAT, lambda: V.tensor_scalar(T.e32[:], T.kdw[:, 0:2048].indirect(T.UL[:, 0:n]), B / 4096.0, -15.0 / 32, OP.mult, OP.add),
-            ["UL"] + ["kd%d" % j for j in range(8)], ["e32"])
-        vec(192, lambda: V.tensor_scalar(T.EL[:], T.e32[:], 2.0, T.s0[:, 0:1], OP.mult, OP.add), ["e32", "s0"], ["EL"])
+        vec(192 * GAT, lambda: V.tensor_scalar(T.EL[:], T.kdw[:, 0:2048].indirect(T.UL[:, 0:n]), B / 4096.0, T.kb[:, 0:1], OP.mult, OP.add),
+            ["UL", "kb"] + ["kd%d" % j for j in range(8)], ["EL"])
 
     kids(0)
     for q, (a, b) in enumerate(((0, 512), (512, 1024), (1024, 1536), (1536, 2048))):
         xk = ["Xq%d" % q] + (["Xs1"] if q == 3 else [])
         vec(256, lambda a=a, b=b: V.tensor_scalar(T.f0s[:, a:b], T.X[:, a:b], T.thf[:, 0:1], -PLAIN, OP.is_lt, OP.mult), xk + ["thf"], ["f0s%d" % q])
-        act(512, lambda a=a, b=b: SC.activation(T.f1s[:, a:b], T.f0s[:, a:b], AF.Identity, bias=1.0, scale=2.0 ** WB / PLAIN), ["f0s%d" % q], ["f1s%d" % q])
-        vec(512, lambda a=a, b=b, q=q: V.tensor_tensor(T.W[:, 2 * a:2 * b:2], ps[q][:], T.f0s[:, a:b], OP.add), ["f0s%d" % q], ["b%d" % q, ("W0s", q)])
-        vec(512, lambda a=a, b=b, q=q: V.tensor_tensor(T.W[:, 2 * a + 1:2 * b:2], ps[q][:], T.f1s[:, a:b], OP.mult), ["f1s%d" % q], ["b%d" % q, ("W1s", q)])
+
+        def wsum(a=a, b=b, q=q):
+            return [PE.matmul(ps[q][:], T.ID[:], T.es[:, a:b], True, False), PE.matmul(ps[q][:], T.ID[:], T.f0s[:, a:b], False, True)]
+        mm(1024, wsum, ["ID", "es%d" % q, "f0s%d" % q], ["b%d" % q])
+        vec(512, lambda a=a, b=b, q=q: V.tensor_tensor(T.W[:, TOT + a:TOT + b], ps[q][:], T.ns[:, a:b], OP.max), ["ns%d" % q], ["b%d" % q, ("W1s", q)])
+        act(512, lambda a=a, b=b, q=q: SC.activation(T.W[:, a:b], ps[q][:], AF.Copy), [], ["b%d" % q, ("W0s", q)])
     vec(WIDE / 2, lambda: V.memset(T.rmax[:], FAR), [], ["rmax"])
     vec(64, lambda: V.memset(T.rmax[:, 0:WIDE:16], -FAR), [], ["rmax"])
     vec(WIDE / 2, lambda: V.memset(T.rmin[:], -FAR), [], ["rmin"])
     vec(64, lambda: V.memset(T.rmin[:, 0:WIDE:16], FAR), [], ["rmin"])
-    gps(0.4, lambda: g.affine_select(T.ID[:], T.ones[:, 0:128], [[-1, 128]], OP.is_equal, 0.0, 0, 1), ["ones"], ["ID"])
-    vec(64, lambda: V.tensor_scalar(T.NI[:], T.ID[:], -1.0, None, OP.mult), ["ID"], ["NI"])
-    vec(64, lambda: V.tensor_scalar(T.HI[:], T.ID[:], 0.5, None, OP.mult), ["ID"], ["HI"])
-    vec(64, lambda: V.memset(T.mh[:], -0.5), [], ["mh"])
-    vec(1, lambda: V.tensor_copy(T.lim[:], T.taui[:]), ["taui"], ["lim"])
+    act(128, lambda: SC.activation(T.NI[:], T.ID[:], AF.Copy, scale=-1.0), ["ID"], ["NI"])
+    act(128, lambda: SC.activation(T.HI[:], T.ID[:], AF.Copy, scale=0.5), ["ID"], ["HI"])
+    fill(T.mh[:], 192, -0.5, "mh")
+    vec(1, lambda: V.tensor_copy(T.tauf[:], T.taui[:]), ["taui"], ["tauf"])
+    fill(T.o16[:], 128, 1.0 / 16, "o16")
+    fill(T.q15[:], 16, -15.0 / 4096, "q15")
     gps(0.4, lambda: g.affine_select(T.ba[:], T.ones[:, 0:128], [[-16, 8], [0, 16]], OP.is_ge, 0.0, 0, 1), ["ones"], ["ba"])
     gps(0.4, lambda: g.affine_select(T.BO[:], T.ba[:], [[16, 8], [0, 16]], OP.is_ge, 0.0, 15, -1), ["ba"], ["BO"])
     gps(0.4, lambda: g.affine_select(T.tr[:], T.BO[:], [[-1, 128]], OP.is_gt, 0.0, 0, 1), ["BO"], ["tr"])
-    vec(64, lambda: V.tensor_scalar(T.TM[:], T.tr[:], -1.0, None, OP.mult), ["tr"], ["TM"])
+    act(128, lambda: SC.activation(T.TM[:], T.tr[:], AF.Copy, scale=-1.0), ["tr"], ["TM"])
     gps(0.15, lambda: g.iota(T.wi[:, 0:12], [[64, 12]], 192, 0, allow_small_or_imprecise_dtypes=True), [], ["wi"])
     vec(1, lambda: V.tensor_scalar(T.s4[:], T.si[:], 4.0, None, OP.mult), ["si"], ["s4"])
     vec(12, lambda: V.tensor_scalar(T.wc[:, 0:12], T.wi[:, 0:12], T.s4[:, 0:1], None, OP.add), ["wi", "s4"], ["wc"])
-    vec(12, lambda: V.memset(T.z12[:], 0.0), [], ["z12"])
-    gps(0.3, lambda: g.iota(T.mio[:], [[0, LASTN // 16], [1, 16]], 0, 0, allow_small_or_imprecise_dtypes=True), [], ["mio"])
+    fill(T.z12[:], 16, 0.0, "z12")
+    gps(0.5, lambda: g.iota(T.mio[:], [[0, 12], [1, 16]], 0, 0, allow_small_or_imprecise_dtypes=True), [], ["mio"])
     vec(1, lambda: V.tensor_copy(T.sf[:], T.si[:]), ["si"], ["sf"])
-    vec(LASTN, lambda: V.tensor_scalar(T.msk[:], T.mio[:], T.sf[:, 0:1], None, OP.is_equal), ["mio", "sf"], ["msk"])
-    for t in range(RO):
-        gps(0.6, lambda t=t: g.iota(T.A[:, 256 * t:256 * t + 256], [[1, 256]], S + 256 * t, 0, allow_small_or_imprecise_dtypes=True), [], [("A", t)])
-        act(256, lambda t=t: SC.activation(T.en[:, 256 * t:256 * t + 256], T.A[:, 256 * t:256 * t + 256], AF.Exp, bias=T.hb[:, 0:1], scale=H), ["hb0", ("A", t)], [("en", t)])
+    vec(NP, lambda: V.tensor_scalar(T.msk[:], T.mio[:], T.sf[:, 0:1], 1.0e6, OP.not_equal, OP.mult), ["mio", "sf"], ["msk"])
+
+    def own(t, late, soon):
+        gps(0.6, lambda: g.iota(T.A[:, 256 * t:256 * t + 256], [[1, 256]], S + 256 * t, 0, allow_small_or_imprecise_dtypes=True), [], [("A", t)], after=late)
+        a = 256 * t + NP
         if t < RO - 1:
-            act(CAP, lambda a=256 * t + NP: SC.activation(T.ng[:, a:a + CAP], T.en[:, a:a + CAP], AF.Copy, scale=-2.0 ** WB), [("en", t)], [("ngm", t)])
-        vec(32, lambda t=t: V.memset(T["mail%d" % t][:, 0:CAP], 0.0), [], [("mail", t)])
-    Wk = [("W%ds" % r, q) for r in range(2) for q in range(4)]
-    Xk = ["Xq0", "Xq1", "Xq2", "Xq3", "Xs1"]
+            act(CAP, lambda: SC.activation(T.ng[:, a:a + CAP], T.en[:, a:a + CAP], AF.Copy, scale=-2.0 ** WB), [("en", t)], [("ngm", t)], after=soon)
+        fill(T["mail%d" % t][:, 0:CAP], CAP, 0.0, ("mail", t))
+
+    for t in range(RO):
+        act(256, lambda t=t: SC.activation(T.en[:, 256 * t:256 * t + 256], T.nam[:, 0:256], AF.Exp, bias=H * (S + 256 * t + 1 - N0), scale=H), ["nam"], [("en", t)])
+    own(0, [], [])
+    for nm, a, b in (("W", S, TOT), ("X", S, N0)):
+        gps(0.2 + 2 * (b - a) * CYC, lambda nm=nm, a=a, b=b: g.iota(T[nm][:, a:b], [[0, b - a]], 0, 0, allow_small_or_imprecise_dtypes=True), [], [nm + "gap"])
+    Wk = ["Wgap"] + [("W%ds" % r, q) for r in range(2) for q in range(4)]
+    Xk = ["Xq0", "Xq1", "Xq2", "Xq3", "Xs1", "Xd", "Xgap"]
     for t in range(RO):
         B = S + t * G
         j0 = t * G
         dfb = 0
-        for gi, grp in enumerate(SG):
-            db = 4 + gi % 2
-            for c in grp:
-                p0, n = CH[c]
-                a, z, w = 16 * p0, 16 * (p0 + n), 16 * n
+        gks = []
+        for c, (p0, n) in enumerate(CH):
+            a, z, w = 16 * p0, 16 * (p0 + n), 16 * n
 
-                def gat(e, a=a, z=z, p0=p0, n=n, B=B):
-                    src = T.W[:, 0:2 * B].indirect(T.EL[:, p0:p0 + n])
+            def gat(e, a=a, z=z, p0=p0, n=n, B=B):
+                src = T.W[:, 0:TOT + B].indirect(T.EL[:, p0:p0 + n])
+                if e == "V":
+                    return [V.tensor_copy(T.gk[:, a:z], src)]
+                return [SC.activation(T.gk[:, a:z], src, AF.Copy)]
+            gks.append(add("VS", w * GAT * CYC + 0.06, gat, ["EL"] + Wk, [("gk", c)]))
+            act(w, lambda a=a, z=z: SC.activation(T.ga[:, a:z], T.gk[:, a:z], AF.Abs), [("gk", c)], [("ga", c)])
+            vec(w / 2, lambda a=a, z=z, w=w: V.tensor_tensor_scan(T.sM[:, a:z], T.rmax[:, 0:w], T.gk[:, a:z], 0.0, OP.min, OP.max), ["rmax", ("gk", c)], [("sM", c)])
+            vec(w / 2, lambda a=a, z=z, w=w: V.tensor_tensor_scan(T.sm[:, a:z], T.rmin[:, 0:w], T.ga[:, a:z], 0.0, OP.max, OP.min), ["rmin", ("ga", c)], [("sm", c)])
+            l0, l1, l2 = 2 * p0, 2 * p0 + n, 2 * (p0 + n)
+            act(n, lambda a=a, z=z, p0=p0, n=n: SC.activation(T.hic[:, p0:p0 + n], T.sM[:, a + 15:z:16], AF.Abs), [("sM", c)], [("hic", c)])
+            act(n, lambda a=a, z=z, l0=l0, l1=l1: SC.activation(T.lh[:, l0:l1], T.sm[:, a + 15:z:16], AF.Ln), [("sm", c)], [("lh", "xl", c)])
+            act(n, lambda l1=l1, l2=l2, p0=p0, n=n: SC.activation(T.lh[:, l1:l2], T.hic[:, p0:p0 + n], AF.Ln), [("hic", c)], [("lh", "xh", c)])
+            vec(2 * n, lambda l0=l0, l2=l2: V.tensor_scalar(T.LH[:, l0:l2], T.lh[:, l0:l2], 1.0 / H, float(N0 - 1), OP.mult, OP.add), [("lh", "xl", c), ("lh", "xh", c)], [("LH", c)])
+            for nm, q0, q1 in (("xh", l1, l2), ("xl", l0, l1)):
+                def gx(e, nm=nm, q0=q0, q1=q1, a=a, z=z, B=B):
+                    src = T.X[:, 0:N0 + B].indirect(T.LH[:, q0:q1])
                     if e == "V":
-                        return [V.tensor_copy(T.gk[:, a:z], src)]
-                    return [SC.activation(T.gk[:, a:z], src, AF.Copy)]
-                add("VS", w * GAT * CYC + 0.06, gat, ["EL"] + Wk, [("gk", c)])
-                act(w, lambda a=a, z=z: SC.activation(T.ga[:, a:z], T.gk[:, a:z], AF.Abs), [("gk", c)], [("ga", c)])
-                vec(w / 2, lambda a=a, z=z, w=w: V.tensor_tensor_scan(T.sM[:, a:z], T.rmax[:, 0:w], T.gk[:, a:z], 0.0, OP.min, OP.max), ["rmax", ("gk", c)], [("sM", c)])
-                vec(n / 2, lambda a=a, z=z, p0=p0, n=n: V.tensor_scalar(T.nrm[:, p0:p0 + n], T.sM[:, a + 15:z:16], 0.0, 2.0 ** -WB, OP.is_ge, OP.max), [("sM", c)], [("nrm", c)])
-                vec(w / 2, lambda a=a, z=z, w=w: V.tensor_tensor_scan(T.sm[:, a:z], T.rmin[:, 0:w], T.ga[:, a:z], 0.0, OP.max, OP.min), ["rmin", ("ga", c)], [("sm", c)])
-                l0, l1, l2 = 2 * p0, 2 * p0 + n, 2 * (p0 + n)
-                vec(2 * n, lambda a=a, z=z, p0=p0, n=n: V.tensor_tensor(T.loc[:, p0:p0 + n], T.sm[:, a + 15:z:16], T.nrm[:, p0:p0 + n], OP.mult), [("sm", c), ("nrm", c)], [("loc", c)])
-                vec(2 * n, lambda a=a, z=z, p0=p0, n=n: V.tensor_tensor(T.hic[:, p0:p0 + n], T.sM[:, a + 15:z:16], T.loc[:, p0:p0 + n], OP.max), [("sM", c), ("loc", c)], [("hic", c)])
-                for nm, cd, q0, q1 in (("xl", "loc", l0, l1), ("xh", "hic", l1, l2)):
-                    act(n, lambda cd=cd, q0=q0, q1=q1, p0=p0, n=n: SC.activation(T.lh[:, q0:q1], T[cd][:, p0:p0 + n], AF.Ln), [(cd, c)], [("lh", nm, c)])
-                vec(2 * n, lambda l0=l0, l2=l2: V.tensor_scalar(T.LH[:, l0:l2], T.lh[:, l0:l2], 1.0 / H, N0 - 1 + 0.245, OP.mult, OP.add), [("lh", "xl", c), ("lh", "xh", c)], [("LH", c)])
-                for nm, q0, q1 in (("xh", l1, l2), ("xl", l0, l1)):
-                    def gx(e, nm=nm, q0=q0, q1=q1, a=a, z=z, B=B):
-                        src = T.X[:, 0:B].indirect(T.LH[:, q0:q1])
-                        if e == "V":
-                            return [V.tensor_copy(T[nm][:, a:z], src)]
-                        return [SC.activation(T[nm][:, a:z], src, AF.Copy)]
-                    add("VS", w * GAT * CYC + 0.06, gx, [("LH", c)] + Xk, [(nm, c)])
-                dk = []
-                for s in range(a, z, 512):
-                    e_ = min(s + 512, z)
-                    if (c, (s - a) // 512) in DV:
-                        vec(2 * (e_ - s), lambda s=s, e_=e_: V.tensor_tensor(T.df[:, s:e_], T.xl[:, s:e_], T.xh[:, s:e_], OP.subtract), [("xl", c), ("xh", c)], [("df", s)])
-                        act(e_ - s, lambda s=s, e_=e_: SC.activation(T.da[:, s:e_], T.df[:, s:e_], AF.Abs), [("df", s)], [("da", s)])
-                        dk.append(("da", s))
-                        continue
+                        return [V.tensor_copy(T[nm][:, a:z], src)]
+                    return [SC.activation(T[nm][:, a:z], src, AF.Copy)]
+                add("VS", w * GAT * CYC + 0.06, gx, [("LH", c)] + Xk, [(nm, c)])
+            dk = []
+            for s in range(a, z, 512):
+                e_ = min(s + 512, z)
+                if (c, (s - a) // 512) in DV:
+                    vec(2 * (e_ - s), lambda s=s, e_=e_: V.tensor_tensor(T.df[:, s:e_], T.xl[:, s:e_], T.xh[:, s:e_], OP.subtract), [("xl", c), ("xh", c)], [("df", s)])
+                    act(e_ - s, lambda s=s, e_=e_: SC.activation(T.da[:, s:e_], T.df[:, s:e_], AF.Abs), [("df", s)], [("da", s)])
+                else:
                     bk = dfb % 4
                     dfb += 1
                     mm(e_ - s, lambda s=s, e_=e_, bk=bk: [PE.matmul(ps[bk][:, 0:e_ - s], T.NI[:], T.xh[:, s:e_], True, False)], ["NI", ("xh", c)], ["b%d" % bk])
                     mm(e_ - s, lambda s=s, e_=e_, bk=bk: [PE.matmul(ps[bk][:, 0:e_ - s], T.ID[:], T.xl[:, s:e_], False, True)], ["ID", ("xl", c)], ["b%d" % bk])
                     act(e_ - s, lambda s=s, e_=e_, bk=bk: SC.activation(T.da[:, s:e_], ps[bk][:, 0:e_ - s], AF.Abs), [], ["b%d" % bk, ("da", s)])
-                    dk.append(("da", s))
+                dk.append(("da", s))
 
-                def dm(a=a, z=z, p0=p0, n=n, db=db):
-                    return [PE.matmul(ps[db][:, p0:p0 + n], T.ZP[:, 15 - p:143 - p], T.da[:, a + p:z:16], p == 0, p == 15) for p in range(16)]
-                mm(16 * max(64, n), dm, ["ZP"] + dk, ["b%d" % db])
-                vec(w / 2, lambda a=a, z=z, w=w: V.tensor_tensor_scan(T.sl[:, a:z], T.rmax[:, 0:w], T.xl[:, a:z], 0.0, OP.min, OP.max), ["rmax", ("xl", c)], [("sl", c)])
-                vec(w / 2, lambda a=a, z=z, w=w: V.tensor_tensor_scan(T.sh[:, a:z], T.rmin[:, 0:w], T.xh[:, a:z], 0.0, OP.max, OP.min), ["rmin", ("xh", c)], [("sh", c)])
-            p0 = CH[grp[0]][0]
-            n = sum(CH[c][1] for c in grp)
-            a, z = 16 * p0, 16 * (p0 + n)
-            vec(n, lambda p0=p0, n=n, db=db: V.tensor_scalar(T.far[:, p0:p0 + n], ps[db][:, p0:p0 + n], T.lim[:, 0:1], None, OP.is_gt), ["lim"], ["b%d" % db, ("far", gi)])
+            def dm(a=a, z=z, p0=p0, n=n):
+                return [PE.matmul(ps[4][:, p0:p0 + n], T.ZP[:, 15 - p:143 - p], T.da[:, a + p:z:16], p == 0, p == 15) for p in range(16)]
+            mm(16 * max(64, n), dm, ["ZP"] + dk, ["b4"])
+            vec(w / 2, lambda a=a, z=z, w=w: V.tensor_tensor_scan(T.sl[:, a:z], T.rmax[:, 0:w], T.xl[:, a:z], 0.0, OP.min, OP.max), ["rmax", ("xl", c)], [("sl", c)])
+            vec(w / 2, lambda a=a, z=z, w=w: V.tensor_tensor_scan(T.sh[:, a:z], T.rmin[:, 0:w], T.xh[:, a:z], 0.0, OP.max, OP.min), ["rmin", ("xh", c)], [("sh", c)])
+        lim = "lim" if t else "tauf"
+        vec(NP, lambda lim=lim: V.tensor_scalar(T.far[:], ps[4][:, 0:NP], T[lim][:, 0:1], None, OP.is_gt), [lim], ["b4", ("far", 0)])
 
-            def xm(a=a, z=z, n=n):
-                o = ps[7][:, 0:n]
-                return [PE.matmul(o, T.HI[:], T.mh[:, 0:n], True, False),
-                        PE.matmul(o, T.HI[:], T.sl[:, a + 15:z:16], False, False),
-                        PE.matmul(o, T.HI[:], T.sh[:, a + 15:z:16], False, True)]
-            mm(3 * max(64, n), xm, ["HI", "mh"] + [(k, c) for c in grp for k in ("sl", "sh")], ["b7"])
-            vec(n, lambda p0=p0, n=n, B=B: V.tensor_scalar(T.X[:, B + p0:B + p0 + n], ps[7][:, 0:n], MAGIC, MAGIC, OP.add, OP.subtract), [], ["b7", ("X", t, gi)])
-            m, c0 = n // 16, p0 // 16
-            last = gi == len(SG) - 1
-            if last:
-                mm(n, lambda p0=p0, n=n: [PE.matmul(ps[6][:, 128:128 + n], T.BO[:], T.far[:, p0:p0 + n], True, True)], ["BO", ("far", gi)], ["b6"])
-                vec(n, lambda n=n: V.tensor_tensor(T.cm[:], ps[6][:, 128:128 + n], T.msk[:], OP.mult), ["msk"], ["b6", "cm"])
-                vec(n / 2, lambda n=n: V.tensor_tensor_scan(T.cs[:], T.rmax[:, 0:n], T.cm[:], 0.0, OP.min, OP.max), ["rmax", "cm"], ["cs"])
-                vec(m, lambda c0=c0, m=m, n=n: V.tensor_scalar(T.Fb[:, c0:c0 + m], T.cs[:, 15:n:16], 1.0, None, OP.is_ge), ["cs"], [("Fb", gi)])
-            else:
-                def cm(p0=p0, n=n, m=m):
-                    return [PE.matmul(ps[6][:, 0:m], T.ZP[:, 15 - s:143 - s], T.far[:, p0 + s:p0 + n:16], s == 0, s == 15) for s in range(16)]
-                mm(16 * 64, cm, ["ZP", ("far", gi)], ["b6"])
-                vec(m, lambda c0=c0, m=m: V.tensor_scalar(T.Fb[:, c0:c0 + m], ps[6][:, 0:m], 1.0, None, OP.is_ge), [], ["b6", ("Fb", gi)])
-            vec(m, lambda c0=c0, m=m: V.tensor_tensor_scan(T.inc[:, c0:c0 + m], T.Fb[:, c0:c0 + m], T.z12[:, 0:m], T.inc[:, c0 - 1:c0] if c0 else 0.0, OP.add, OP.max),
-                ["z12", ("Fb", gi)] + ([("inc", gi - 1)] if c0 else []), [("inc", gi)])
-            vec(2 * m, lambda c0=c0, m=m: V.tensor_tensor(T.Fw[:, c0:c0 + m], T.Fb[:, c0:c0 + m], T.wc[:, c0:c0 + m], OP.mult), ["wc", ("Fb", gi)], [("Fw", gi)])
-
-            def cu(c0=c0, m=m):
-                o = ps[6][:, 32:32 + m]
-                return [PE.matmul(o, T.ID[:], T.wc[:, c0:c0 + m], True, False),
-                        PE.matmul(o, T.TM[:], T.Fb[:, c0:c0 + m], False, False),
-                        PE.matmul(o, T.BO[:], T.inc[:, c0:c0 + m], False, False),
-                        PE.matmul(o, T.NI[:], T.Fw[:, c0:c0 + m], False, True)]
-            mm(4 * 64, cu, ["ID", "TM", "BO", "NI", "wc", ("Fb", gi), ("inc", gi), ("Fw", gi)], ["b6"])
-            vec(m, lambda c0=c0, m=m: V.tensor_scalar(T.slots[:, c0:c0 + m], ps[6][:, 32:32 + m], -1.0, None, OP.add), [], ["b6", ("slots", gi)])
-            vec(3.5 * n, lambda c0=c0, m=m, p0=p0, n=n, B=B, t=t: V.tensor_copy(T["mail%d" % t][:, 0:MW].indirect(T.slots[:, c0:c0 + m]), T.X[:, B + p0:B + p0 + n]),
-                [("slots", gi), ("X", t, gi)], [("mail", t)])
+        def xm():
+            o = ps[7][:, 0:NP]
+            return [PE.matmul(o, T.HI[:], T.mh[:], True, False),
+                    PE.matmul(o, T.HI[:], T.sl[:, 15:16 * NP:16], False, False),
+                    PE.matmul(o, T.HI[:], T.sh[:, 15:16 * NP:16], False, True)]
+        mm(3 * NP, xm, ["HI", "mh"] + [(k, c) for c in range(NCH) for k in ("sl", "sh")], ["b7"])
+        vec(NP, lambda B=B: V.tensor_scalar(T.X[:, B:B + NP], ps[7][:, 0:NP], MAGIC, MAGIC, OP.add, OP.subtract), [], ["b7", "Xgap", ("X", t, 0)])
+        m = 12
+        mm(NP, lambda: [PE.matmul(ps[6][:, 128:128 + NP], T.BO[:], T.far[:], True, True)], ["BO", ("far", 0)], ["b6"])
+        vec(NP, lambda: V.tensor_tensor(T.cm[:], ps[6][:, 128:128 + NP], T.msk[:], OP.is_gt), ["msk"], ["b6", "cm"])
+        vec(NP / 2, lambda: V.tensor_tensor_scan(T.cs[:], T.rmax[:, 0:NP], T.cm[:], 0.0, OP.min, OP.max), ["rmax", "cm"], ["cs"])
+        F = T.cs[:, 15:NP:16]
+        vec(m, lambda F=F: V.tensor_tensor_scan(T.inc[:, 0:m], F, T.z12[:, 0:m], 0.0, OP.add, OP.max), ["z12", "cs"], [("inc", 0)])
+        vec(2 * m, lambda F=F: V.tensor_tensor(T.Fw[:, 0:m], F, T.wc[:, 0:m], OP.mult), ["wc", "cs"], [("Fw", 0)])
+        o6 = ps[6][:, 32:32 + m]
+        mm(128, lambda F=F, o6=o6: [PE.matmul(o6, T.ID[:], T.wc[:, 0:m], True, False), PE.matmul(o6, T.TM[:], F, False, False)], ["ID", "TM", "wc", "cs"], ["b6"])
+        mm(64, lambda o6=o6: [PE.matmul(o6, T.BO[:], T.inc[:, 0:m], False, False)], ["BO", ("inc", 0)], ["b6"])
+        mm(64, lambda o6=o6: [PE.matmul(o6, T.NI[:], T.Fw[:, 0:m], False, True)], ["NI", ("Fw", 0)], ["b6"])
+        vec(m, lambda o6=o6: V.tensor_scalar(T.slots[:, 0:m], o6, -1.0, None, OP.add), [], ["b6", ("slots", 0)])
+        vec(3.5 * NP, lambda B=B, t=t: V.tensor_copy(T["mail%d" % t][:, 0:MW].indirect(T.slots[:, 0:m]), T.X[:, B:B + NP]), [("slots", 0), ("X", t, 0)], [("mail", t)])
+        scat = lastw[("mail", t)]
         dst = T.cores[(rank + 1 + t % (len(T.cores) - 1)) % len(T.cores)]
         eng = topo.engines(core, dst)[:8]
         msk = sum(1 << e for e in eng)
         rid, pid = topo.addr(dst)[:2]
         ne = len(eng)
         m0, m1 = B + NP, B + G
-        snd = add("G", 1.0, lambda e, t=t, m0=m0, m1=m1, rid=rid, pid=pid, msk=msk: [g.remote_dma(T.X[:, m0:m1], T["mail%d" % t][:, 0:CAP], T.sem["arr%d" % t], T.sem.sent, pid, rid, msk)],
+        snd = add("G", 1.0, lambda e, t=t, rid=rid, pid=pid, msk=msk: [g.remote_dma(T["min%d" % t][:], T["mail%d" % t][:, 0:CAP], T.sem["arr%d" % t], T.sem.sent, pid, rid, msk)],
                   [("mail", t)], [], sem="sent", val=ne)
-        add("R", 0.0, None, [], [("X", t, "m")], lat=MAILT, sem="arr%d" % t, val=ne, after=[snd])
-        nl = [("loc", c) for c in range(NCH)]
-        nf = [("far", k) for k in range(len(SG))]
-        nx = [("X", t, k) for k in range(len(SG))]
-        vec(2 * NP, lambda j0=j0: V.tensor_tensor(T.fn[:], T.far[:], T.en[:, j0:j0 + NP], OP.mult), nf + [("en", t)], ["fn"])
-        vec(2 * NP, lambda j0=j0: V.tensor_tensor(T.en[:, j0:j0 + NP], T.loc[:], T.fn[:], OP.max), nl + ["fn"], [("en", t)])
+        arr = add("R", 0.0, None, [], [("min", t)], lat=MAILT, sem="arr%d" % t, val=ne, after=[snd])
+        if t < RO - 1:
+            def cp(a, b, src, rd):
+                gps(0.2 + 2 * (b - a) * CYC, lambda: g.affine_select(T.X[:, a:b], src, [[0, b - a]], OP.is_equal, 0.0, 0, 0), rd, ["Xgap"])
+            cp(N0 + B, N0 + B + NP, T.X[:, B:B + NP], [("X", t, 0), ("mail", t)])
+            cp(m0, m1, T["min%d" % t][:], [("min", t)])
+            cp(N0 + m0, N0 + m1, T["min%d" % t][:], [("min", t)])
+        nl = [(k, c) for c in range(NCH) for k in ("sM", "sm")]
+        mm(NP, lambda j0=j0: [PE.matmul(ps[5][:, 0:NP], T.ID[:], T.en[:, j0:j0 + NP], True, True)], ["ID", ("en", t)], ["b5"])
+        vec(NP, lambda: V.tensor_tensor(T.fn[:], ps[5][:, 0:NP], T.far[:], OP.mult), [("far", 0)], ["b5", "fn"])
+        act(NP, lambda: SC.activation(T.nrm[:], T.sM[:, 15:16 * NP:16], AF.Sign), nl, ["nrm"])
+        act(NP, lambda: SC.activation(ps[0][:, 0:NP], T.nrm[:], AF.Relu), ["nrm"], ["b0"])
+        act(NP, lambda: SC.activation(T.c0[:], T.sM[:, 15:16 * NP:16], AF.Relu, scale=-2.0 ** -WB), nl, ["c0"])
+        vec(NP, lambda: V.tensor_tensor(T.loc[:], ps[0][:, 0:NP], T.sm[:, 15:16 * NP:16], OP.mult), nl, ["b0", "loc"])
+
+        def ls():
+            o = ps[5][:, 256:256 + NP]
+            return [PE.matmul(o, T.ID[:], T.loc[:], True, False), PE.matmul(o, T.ID[:], T.c0[:], False, True)]
+        mm(2 * NP, ls, ["ID", "c0", "loc"], ["b5"])
+        vec(NP, lambda j0=j0: V.tensor_tensor(T.en[:, j0:j0 + NP], ps[5][:, 256:256 + NP], T.fn[:], OP.max), ["fn"], ["b5", ("en", t)])
         act(NP, lambda j0=j0: SC.activation(T.ln1[:], T.en[:, j0:j0 + NP], AF.Ln), [("en", t)], ["ln1"])
         act(NP, lambda: SC.activation(T.ln2[:], T.ln1[:], AF.Identity, bias=MAGIC + N0 - 1, scale=1.0 / H), ["ln1"], ["ln2"])
         act(NP, lambda j0=j0: SC.activation(T.A[:, j0:j0 + NP], T.ln2[:], AF.Identity, bias=-MAGIC), ["ln2"], [("A", t)])
         if t < RO - 1:
             kids(t + 1)
-            for lab, q0, q1, rd in (("p", 0, NP, nx), ("m", NP, G, [("X", t, "m")])):
-                vec((q1 - q0) / 2, lambda B=B, q0=q0, q1=q1: V.tensor_scalar(T.f0[:, q0:q1], T.X[:, B + q0:B + q1], T.thf[:, 0:1], -PLAIN, OP.is_lt, OP.mult), rd + ["thf"], ["f0" + lab])
-                if lab == "p":
-                    act(NP, lambda j0=j0: SC.activation(T.ng[:, j0:j0 + NP], T.en[:, j0:j0 + NP], AF.Copy, scale=-2.0 ** WB), [("en", t)], [("ngp", t)])
-                w0, w1, wz = 2 * (B + q0), 2 * (B + q0) + 1, 2 * (B + q1)
-                vec(2 * (q1 - q0), lambda q0=q0, q1=q1, w0=w0, wz=wz, j0=j0: V.tensor_tensor(T.W[:, w0:wz:2], T.en[:, j0 + q0:j0 + q1], T.f0[:, q0:q1], OP.add),
-                    [("en", t), "f0" + lab], [("W", t, "0" + lab)])
-                vec(2 * (q1 - q0), lambda q0=q0, q1=q1, w0=w0, w1=w1, wz=wz, j0=j0: V.tensor_tensor(T.W[:, w1:wz:2], T.ng[:, j0 + q0:j0 + q1], T.W[:, w0:wz:2], OP.max),
-                    [("ng" + lab, t), ("W", t, "0" + lab)], [("W", t, "1" + lab)])
-                Wk += [("W", t, "0" + lab), ("W", t, "1" + lab)]
-            Xk += nx + [("X", t, "m")]
-            mm(64, lambda: [PE.matmul(ps[6][:, 64:65], T.ones[:, 0:128], T.inc[:, 11:12], True, True)], ["ones", ("inc", len(SG) - 1)], ["b6"])
-            vec(1, lambda: V.tensor_copy(T.ci[:], ps[6][:, 64:65]), [], ["b6", "ci"])
-            vec(1, lambda: V.tensor_scalar(T.cj[:], T.ci[:], 15, None, OP.bitwise_and), ["ci"], ["cj"])
-            vec(1, lambda: V.tensor_tensor(T.lim[:], T.taui[:], T.cj[:], OP.add), ["cj", "taui"], ["lim"])
-        dma("Y", T.yx[:, j0:j0 + NP], T.X[:, B:B + NP], nx, [])
-        dma("Y", T.ya[:, j0:j0 + G], T.A[:, j0:j0 + G], [("A", t)], [])
-        dma("Y", T.yx[:, j0 + NP:j0 + G], T.X[:, B + NP:B + G], [("X", t, "m")], [])
+            vec(NP / 2, lambda B=B: V.tensor_scalar(T.f0[:, 0:NP], T.X[:, B:B + NP], T.thf[:, 0:1], -PLAIN, OP.is_lt, OP.mult), [("X", t, 0), "thf"], ["f0p"])
+            act(NP, lambda j0=j0: SC.activation(T.ng[:, j0:j0 + NP], T.en[:, j0:j0 + NP], AF.Copy, scale=-2.0 ** WB), [("en", t)], [("ngp", t)])
+
+            def ws(j0=j0):
+                o = ps[4][:, 256:256 + NP]
+                return [PE.matmul(o, T.ID[:], T.en[:, j0:j0 + NP], True, False), PE.matmul(o, T.ID[:], T.f0[:, 0:NP], False, True)]
+            mm(2 * NP, ws, ["ID", ("en", t), "f0p"], ["b4"])
+            vec(NP, lambda B=B, j0=j0: V.tensor_tensor(T.W[:, TOT + B:TOT + B + NP], ps[4][:, 256:256 + NP], T.ng[:, j0:j0 + NP], OP.max), [("ngp", t)], ["b4", ("W", t, "1p")])
+            act(NP, lambda B=B: SC.activation(T.W[:, B:B + NP], ps[4][:, 256:256 + NP], AF.Copy), [], ["b4", ("W", t, "0p")])
+            vec(CAP / 2, lambda t=t: V.tensor_scalar(T.f0[:, NP:G], T["min%d" % t][:], T.thf[:, 0:1], -PLAIN, OP.is_lt, OP.mult), [("min", t), "thf"], ["f0m"])
+            add("V", 2 * CAP * CYC + FIX["V"], lambda e, B=B, j0=j0: [V.tensor_tensor(T.W[:, B + NP:B + G], T.en[:, j0 + NP:j0 + G], T.f0[:, NP:G], OP.add)],
+                [("en", t), "f0m"], [("W", t, "0m")], after=gks)
+            vec(2 * CAP, lambda B=B, j0=j0: V.tensor_tensor(T.W[:, TOT + B + NP:TOT + B + G], T.ng[:, j0 + NP:j0 + G], T.W[:, B + NP:B + G], OP.max),
+                [("ngm", t), ("W", t, "0m")], [("W", t, "1m")])
+            Wk += [("W", t, k) for k in ("0p", "1p", "0m", "1m")]
+            Xk += [("X", t, 0)]
+
+            def cc():
+                return [PE.matmul(ps[6][:, 64:65], T.ones[:, 0:128], T.inc[:, 11:12], True, True),
+                        PE.matmul(ps[6][:, 66:67], T.o16[:], T.inc[:, 11:12], True, False),
+                        PE.matmul(ps[6][:, 66:67], T.ones[:, 0:128], T.q15[:, 0:1], False, True)]
+            mm(192, cc, ["ones", "o16", "q15", ("inc", 0)], ["b6"])
+            own(t + 1, [arr], [scat])
+            act(1, lambda: SC.activation(T.cf[:], ps[6][:, 66:67], AF.Identity, bias=MAGIC), [], ["b6", "cf"])
+            act(1, lambda: SC.activation(T.tc[:], ps[6][:, 64:65], AF.Identity, bias=T.tauf[:, 0:1]), ["tauf"], ["b6", "tc"])
+            act(1, lambda: SC.activation(T.cg[:], T.cf[:], AF.Identity, bias=-MAGIC), ["cf"], ["cg"])
+            act(1, lambda: SC.activation(T.lim[:], T.cg[:], AF.Identity, bias=T.tc[:, 0:1], scale=-16.0), ["cg", "tc"], ["lim"])
+        dma(T.yx[:, j0:j0 + NP], T.X[:, B:B + NP], [("X", t, 0)], [])
+        dma(T.ya[:, j0:j0 + G], T.A[:, j0:j0 + G], [("A", t)], [])
+        dma(T.yx[:, j0 + NP:j0 + G], T["min%d" % t][:], [("min", t)], [])
     emit_all(g, T, tasks)
 
 
@@ -400,9 +384,9 @@ def plan(tasks):
         for i in avail:
             for q in tasks[i]["eng"]:
                 st = ready[i] if q == "R" else max(free[q], ready[i])
-                cand.append((st + (VPEN if q == "V" and tasks[i]["eng"] == "VS" else 0.0), -prio[i], i, q, st))
+                cand.append((st, -prio[i], i, q))
         first = min(cand)
-        _, i, q, st = min(x[1:] for x in cand if x[3] == first[3] and x[0] <= first[0] + SLACK)
+        _, i, q, st = min((x[1], x[2], x[3], x[0]) for x in cand if x[3] == first[3] and x[0] <= first[0] + SLACK)
         avail.discard(i)
         k = tasks[i]
         end = st + k["cost"]

import math
from concourse.mybir import dt, AluOpType, AxisListType, ActivationFunctionType

S, NP, CAP, RO, G = 2048, 192, 64, 5, 256
TOT = S + RO * G
CH = [(0, 64), (64, 64), (128, 64)]
GE = {"Vgk0": "V", "Vgk2": "V", "Vxh0": "V", "Vxh1": "S", "Vxl0": "S", "Vxl1": "V", "Vxl2": "S"}
PRI = {"Sc0": 6, "Vfn": -3, "Vsh2": -6, "VUL": -12, "Vxl0": -12, "Sda2048": 6, "Sda2560": 3, "VW1s1": -12, "Sda0": 12, "Vkl": -6,
       "Vwc": -1.5, "VW1s0": -3, "Vtauf": -3, "Vmsk": -3, "VZW": -3, "Sen": 20}
DV = [(2, 1)]
NCH = len(CH)
WIDE = 16 * max(n for _, n in CH)
N0 = 3336
WB = 63
H = WB * math.log(2.0) / N0
PLAIN = 2.0 ** 99
FAR = 9.0e29
MW = 1152
MAGIC = 12582912.0

SCRATCH = {
    "X": ("sbuf", [128, N0 + TOT], "bfloat16"),
    "W": ("sbuf", [128, 2 * TOT], "bfloat16"),
    "kdw": ("sbuf", [128, 2048], "int32"),
    "nam": ("sbuf", [128, 512], "float32"),
    "A": ("sbuf", [128, RO * G], "float32"),
    "en": ("sbuf", [128, RO * G], "bfloat16"),
    "ng": ("sbuf", [128, RO * G], "bfloat16"),
    "es": ("sbuf", [128, 2048], "bfloat16"),
    "ns": ("sbuf", [128, 2048], "bfloat16"),
    "f0s": ("sbuf", [128, 2048], "bfloat16"),
    "f0": ("sbuf", [128, 256], "bfloat16"),
    "kb": ("sbuf", [128, 1], "float32"),
    "UL": ("sbuf", [128, 16], "uint16"),
    "EL": ("sbuf", [128, 192], "uint16"),
    "lh": ("sbuf", [128, 384], "float32"),
    "LH": ("sbuf", [128, 384], "uint16"),
    "ln1": ("sbuf", [128, 192], "float32"),
    "ln2": ("sbuf", [128, 192], "float32"),
    "ZP": ("sbuf", [128, 144], "bfloat16"),
    "slots": ("sbuf", [128, 16], "uint16"),
}
for _k in ("gk", "ga", "sM", "sm", "xl", "xh", "sl", "sh", "df", "da"):
    SCRATCH[_k] = ("sbuf", [128, 16 * NP], "bfloat16")
for _k in ("nrm", "c0", "loc", "hic", "far", "fn", "cm", "cs", "msk", "mh"):
    SCRATCH[_k] = ("sbuf", [128, NP], "bfloat16")
for _k in ("rmax", "rmin"):
    SCRATCH[_k] = ("sbuf", [128, WIDE], "bfloat16")
for _k in ("ones", "za", "zb", "ZW"):
    SCRATCH[_k] = ("sbuf", [128, 144], "bfloat16")
for _k in ("ba", "BO", "tr", "TM", "ID", "NI", "HI", "o16"):
    SCRATCH[_k] = ("sbuf", [128, 128], "bfloat16")
for _k in ("wc", "inc", "Fw", "z12", "q15"):
    SCRATCH[_k] = ("sbuf", [128, 16], "bfloat16")
for _k in ("u1", "u2", "ki", "kj", "kl"):
    SCRATCH[_k] = ("sbuf", [128, 16], "int32")
for _k in ("k613", "wi"):
    SCRATCH[_k] = ("sbuf", [128, 16], "float32")
SCRATCH["mio"] = ("sbuf", [128, NP], "float32")
for _k in ("pi", "si", "wti", "thi", "taui"):
    SCRATCH[_k] = ("sbuf", [128, 1], "int32")
for _k in ("s0", "s4", "s613", "sf", "wtf", "thf", "tauf", "lim", "cf", "cg", "tc"):
    SCRATCH[_k] = ("sbuf", [128, 1], "float32")
for _t in range(RO):
    SCRATCH["min%d" % _t] = ("sbuf", [128, CAP], "bfloat16")
    SCRATCH["mail%d" % _t] = ("sbuf", [128, MW], "bfloat16")
for _b in range(8):
    SCRATCH["ps%d" % _b] = ("psum", [128, 512], "float32")

SEMAPHORES = ["cV", "cS", "cP", "cG", "sent"] + ["arr%d" % t for t in range(RO)] + ["d%d" % i for i in range(40)]

CYC = 0.00083 * 1.05
GAT = 1.4
FIX = {"V": 0.04, "S": 0.07, "P": 0.03, "G": 0.2, "Y": 0.1}
WAKE = 0.08
MAILT = 2.0
SLACK = 0.2


def rank_program(g, core, T, topo):
    rank = T.rank_of(core)
    if rank is None:
        return
    AF, OP = ActivationFunctionType, AluOpType
    V, SC, PE = g.vector, g.scalar, g.tensor
    ps = [T["ps%d" % b] for b in range(8)]
    tasks, lastw, readers = [], {}, {}

    def add(eng, cost, emit, rd=(), wr=(), lat=0.0, sem=None, val=0, after=()):
        i = len(tasks)
        deps = set(after)
        for k in rd:
            if k in lastw:
                deps.add(lastw[k])
        for k in wr:
            if k in lastw:
                deps.add(lastw[k])
            deps.update(readers.get(k, ()))
        for k in wr:
            lastw[k] = i
            readers[k] = []
        for k in rd:
            if k not in wr:
                readers.setdefault(k, []).append(i)
        deps.discard(i)
        k = (rd if eng == "P" else wr or ["out"])[-1]
        lab = eng[0] + (k if isinstance(k, str) else k[0] + ("" if k[0] in ("mail", "A", "en") else str(k[-1])))
        tasks.append(dict(eng=GE.get(lab, eng), cost=cost, emit=emit, deps=sorted(deps), lat=lat, sem=sem, val=val, lab=lab))
        return i

    nd = [0]

    def dma(out, in_, rd, wr, lat=2.5):
        name = "d%d" % nd[0]
        nd[0] += 1
        add("Y", 0.06, lambda e: [g.sync.dma_start(out, in_)], rd, wr, lat, name, 16)

    def vec(cyc, emit, rd, wr):
        add("V", max(64, cyc) * CYC + FIX["V"], lambda e: [emit()], rd, wr)

    def act(cyc, emit, rd, wr, after=()):
        add("S", cyc * CYC + FIX["S"], lambda e: [emit()], rd, wr, after=after)

    def mm(cyc, emit, rd, wr):
        add("P", cyc * CYC + FIX["P"], lambda e: emit(), rd, wr)

    def gps(cost, emit, rd, wr, after=()):
        add("G", cost, lambda e: [emit()], rd, wr, after=after)

    dma(T.wti[:], T.wt[:], [], ["wti"])
    dma(T.X[:, 1792:2048], T.x0[:, 1792:2048], [], ["Xs1"])
    dma(T.thi[:], T.th[:], [], ["thi"])
    for q, (a, b) in enumerate(((0, 512), (512, 1024), (1024, 1536), (1536, 1792))):
        dma(T.X[:, a:b], T.x0[:, a:b], [], ["Xq%d" % q], 2.6 + 0.7 * q)
    for j in range(8):
        dma(T.kdw[16 * j:16 * j + 16, :], T.kd[:], [], ["kd%d" % j], 4.0 + 0.6 * j)
    dma(T.taui[:], T.tau[:], [], ["taui"], 6.0)
    dma(T.X[:, N0:N0 + S], T.x0[:], [], ["Xd"], 9.0)
    vec(72, lambda: V.memset(T.ones[:], 1.0), [], ["ones"])
    gps(1.0, lambda: g.iota(T.nam[:], [[1, 512]], 0, 0, allow_small_or_imprecise_dtypes=True), [], ["nam"])
    gps(0.4, lambda: g.affine_select(T.ID[:], T.ones[:, 0:128], [[-1, 128]], OP.is_equal, 0.0, 0, 1), ["ones"], ["ID"])
    for q in range(4):
        a, b = 512 * q, 512 * q + 512
        act(512, lambda a=a, b=b: SC.activation(T.es[:, a:b], T.nam[:], AF.Exp, bias=H * (a + 1 - N0), scale=H), ["nam"], ["es%d" % q])
    for q in range(4):
        a, b = 512 * q, 512 * q + 512
        act(512, lambda a=a, b=b: SC.activation(T.ns[:, a:b], T.es[:, a:b], AF.Copy, scale=-2.0 ** WB), ["es%d" % q], ["ns%d" % q])
    gps(0.15, lambda: g.iota(T.pi[:], [[1, 1]], 0, 1), [], ["pi"])

    def fill(out, n, value, key):
        act(n, lambda: SC.activation(out, T.nam[:, 0:n], AF.Identity, bias=value, scale=0.0), ["nam"], [key])
    gps(0.15, lambda: g.iota(T.ki[:, 0:12], [[16 * 613, 12]], 0, 0), [], ["ki"])
    gps(0.4, lambda: g.affine_select(T.za[:], T.ones[:], [[0, 9], [1, 16]], OP.is_equal, 0.0, -15, 0), ["ones"], ["za"])
    gps(0.4, lambda: g.affine_select(T.zb[:], T.za[:], [[-16, 9], [0, 16]], OP.is_ge, 0.0, 0, 1), ["za"], ["zb"])
    gps(0.4, lambda: g.affine_select(T.ZP[:], T.zb[:], [[16, 9], [0, 16]], OP.is_ge, 0.0, 15, -1), ["zb"], ["ZP"])
    vec(1, lambda: V.tensor_copy(T.wtf[:], T.wti[:]), ["wti"], ["wtf"])
    vec(72, lambda: V.tensor_scalar(T.ZW[:], T.ZP[:], T.wtf[:, 0:1], None, OP.mult), ["ZP", "wtf"], ["ZW"])
    vec(1, lambda: V.tensor_scalar(T.si[:], T.pi[:], 15, None, OP.bitwise_and), ["pi"], ["si"])
    vec(1, lambda: V.tensor_scalar(T.s613[:], T.si[:], 613.0, None, OP.mult), ["si"], ["s613"])
    vec(12, lambda: V.tensor_scalar(T.kj[:, 0:12], T.ki[:, 0:12], T.s613[:, 0:1], None, OP.add), ["ki", "s613"], ["kj"])
    vec(12, lambda: V.tensor_scalar(T.kl[:, 0:12], T.kj[:, 0:12], 2047, None, OP.bitwise_and), ["kj"], ["kl"])
    vec(12, lambda: V.tensor_copy(T.k613[:, 0:12], T.kl[:, 0:12]), ["kl"], ["k613"])
    vec(1, lambda: V.tensor_scalar(T.s0[:], T.si[:], 0.0, float(TOT), OP.is_equal, OP.mult), ["si"], ["s0"])
    vec(1, lambda: V.tensor_scalar(T.kb[:], T.s0[:], 15.0 / 32, None, OP.subtract), ["s0"], ["kb"])
    vec(1, lambda: V.tensor_copy(T.thf[:], T.thi[:]), ["thi"], ["thf"])

    def kids(t):
        B = S + t * G
        b = B - G
        src = ["Xs1"] if t == 0 else [("X", t - 1, 0)]
        n = 12

        def um():
            return [PE.matmul(ps[7][:, 256:256 + n], T.ZW[:, 15 - s:143 - s], T.X[:, b + s:b + NP:16], s == 0, s == 15) for s in range(16)]
        mm(16 * 64, um, ["ZW"] + src, ["b7"])
        vec(12, lambda: V.tensor_tensor(T.u1[:, 0:n], ps[7][:, 256:256 + n], T.k613[:, 0:n], OP.add), ["k613"], ["b7", "u1"])
        vec(12, lambda: V.tensor_scalar(T.u2[:, 0:n], T.u1[:, 0:n], 2047, None, OP.bitwise_and), ["u1"], ["u2"])
        vec(12, lambda: V.tensor_copy(T.UL[:, 0:n], T.u2[:, 0:n]), ["u2"], ["UL"])
        vec(192 * GAT, lambda: V.tensor_scalar(T.EL[:], T.kdw[:, 0:2048].indirect(T.UL[:, 0:n]), B / 4096.0, T.kb[:, 0:1], OP.mult, OP.add),
            ["UL", "kb"] + ["kd%d" % j for j in range(8)], ["EL"])

    kids(0)
    for q, (a, b) in enumerate(((0, 512), (512, 1024), (1024, 1536), (1536, 2048))):
        xk = ["Xq%d" % q] + (["Xs1"] if q == 3 else [])
        vec(256, lambda a=a, b=b: V.tensor_scalar(T.f0s[:, a:b], T.X[:, a:b], T.thf[:, 0:1], -PLAIN, OP.is_lt, OP.mult), xk + ["thf"], ["f0s%d" % q])

        def wsum(a=a, b=b, q=q):
            return [PE.matmul(ps[q][:], T.ID[:], T.es[:, a:b], True, False), PE.matmul(ps[q][:], T.ID[:], T.f0s[:, a:b], False, True)]
        mm(1024, wsum, ["ID", "es%d" % q, "f0s%d" % q], ["b%d" % q])
        vec(512, lambda a=a, b=b, q=q: V.tensor_tensor(T.W[:, TOT + a:TOT + b], ps[q][:], T.ns[:, a:b], OP.max), ["ns%d" % q], ["b%d" % q, ("W1s", q)])
        act(512, lambda a=a, b=b, q=q: SC.activation(T.W[:, a:b], ps[q][:], AF.Copy), [], ["b%d" % q, ("W0s", q)])
    vec(WIDE / 2, lambda: V.memset(T.rmax[:], FAR), [], ["rmax"])
    vec(64, lambda: V.memset(T.rmax[:, 0:WIDE:16], -FAR), [], ["rmax"])
    vec(WIDE / 2, lambda: V.memset(T.rmin[:], -FAR), [], ["rmin"])
    vec(64, lambda: V.memset(T.rmin[:, 0:WIDE:16], FAR), [], ["rmin"])
    act(128, lambda: SC.activation(T.NI[:], T.ID[:], AF.Copy, scale=-1.0), ["ID"], ["NI"])
    act(128, lambda: SC.activation(T.HI[:], T.ID[:], AF.Copy, scale=0.5), ["ID"], ["HI"])
    fill(T.mh[:], 192, -0.5, "mh")
    vec(1, lambda: V.tensor_copy(T.tauf[:], T.taui[:]), ["taui"], ["tauf"])
    fill(T.o16[:], 128, 1.0 / 16, "o16")
    fill(T.q15[:], 16, -15.0 / 4096, "q15")
    gps(0.4, lambda: g.affine_select(T.ba[:], T.ones[:, 0:128], [[-16, 8], [0, 16]], OP.is_ge, 0.0, 0, 1), ["ones"], ["ba"])
    gps(0.4, lambda: g.affine_select(T.BO[:], T.ba[:], [[16, 8], [0, 16]], OP.is_ge, 0.0, 15, -1), ["ba"], ["BO"])
    gps(0.4, lambda: g.affine_select(T.tr[:], T.BO[:], [[-1, 128]], OP.is_gt, 0.0, 0, 1), ["BO"], ["tr"])
    act(128, lambda: SC.activation(T.TM[:], T.tr[:], AF.Copy, scale=-1.0), ["tr"], ["TM"])
    gps(0.15, lambda: g.iota(T.wi[:, 0:12], [[64, 12]], 192, 0, allow_small_or_imprecise_dtypes=True), [], ["wi"])
    vec(1, lambda: V.tensor_scalar(T.s4[:], T.si[:], 4.0, None, OP.mult), ["si"], ["s4"])
    vec(12, lambda: V.tensor_scalar(T.wc[:, 0:12], T.wi[:, 0:12], T.s4[:, 0:1], None, OP.add), ["wi", "s4"], ["wc"])
    fill(T.z12[:], 16, 0.0, "z12")
    gps(0.5, lambda: g.iota(T.mio[:], [[0, 12], [1, 16]], 0, 0, allow_small_or_imprecise_dtypes=True), [], ["mio"])
    vec(1, lambda: V.tensor_copy(T.sf[:], T.si[:]), ["si"], ["sf"])
    vec(NP, lambda: V.tensor_scalar(T.msk[:], T.mio[:], T.sf[:, 0:1], 1.0e6, OP.not_equal, OP.mult), ["mio", "sf"], ["msk"])

    def own(t, late, soon):
        gps(0.6, lambda: g.iota(T.A[:, 256 * t:256 * t + 256], [[1, 256]], S + 256 * t, 0, allow_small_or_imprecise_dtypes=True), [], [("A", t)], after=late)
        a = 256 * t + NP
        if t < RO - 1:
            act(CAP, lambda: SC.activation(T.ng[:, a:a + CAP], T.en[:, a:a + CAP], AF.Copy, scale=-2.0 ** WB), [("en", t)], [("ngm", t)], after=soon)
        fill(T["mail%d" % t][:, 0:CAP], CAP, 0.0, ("mail", t))

    for t in range(RO):
        act(256, lambda t=t: SC.activation(T.en[:, 256 * t:256 * t + 256], T.nam[:, 0:256], AF.Exp, bias=H * (S + 256 * t + 1 - N0), scale=H), ["nam"], [("en", t)])
    own(0, [], [])
    for nm, a, b in (("W", S, TOT), ("X", S, N0)):
        gps(0.2 + 2 * (b - a) * CYC, lambda nm=nm, a=a, b=b: g.iota(T[nm][:, a:b], [[0, b - a]], 0, 0, allow_small_or_imprecise_dtypes=True), [], [nm + "gap"])
    Wk = ["Wgap"] + [("W%ds" % r, q) for r in range(2) for q in range(4)]
    Xk = ["Xq0", "Xq1", "Xq2", "Xq3", "Xs1", "Xd", "Xgap"]
    for t in range(RO):
        B = S + t * G
        j0 = t * G
        dfb = 0
        gks = []
        for c, (p0, n) in enumerate(CH):
            a, z, w = 16 * p0, 16 * (p0 + n), 16 * n

            def gat(e, a=a, z=z, p0=p0, n=n, B=B):
                src = T.W[:, 0:TOT + B].indirect(T.EL[:, p0:p0 + n])
                if e == "V":
                    return [V.tensor_copy(T.gk[:, a:z], src)]
                return [SC.activation(T.gk[:, a:z], src, AF.Copy)]
            gks.append(add("VS", w * GAT * CYC + 0.06, gat, ["EL"] + Wk, [("gk", c)]))
            act(w, lambda a=a, z=z: SC.activation(T.ga[:, a:z], T.gk[:, a:z], AF.Abs), [("gk", c)], [("ga", c)])
            vec(w / 2, lambda a=a, z=z, w=w: V.tensor_tensor_scan(T.sM[:, a:z], T.rmax[:, 0:w], T.gk[:, a:z], 0.0, OP.min, OP.max), ["rmax", ("gk", c)], [("sM", c)])
            vec(w / 2, lambda a=a, z=z, w=w: V.tensor_tensor_scan(T.sm[:, a:z], T.rmin[:, 0:w], T.ga[:, a:z], 0.0, OP.max, OP.min), ["rmin", ("ga", c)], [("sm", c)])
            l0, l1, l2 = 2 * p0, 2 * p0 + n, 2 * (p0 + n)
            act(n, lambda a=a, z=z, p0=p0, n=n: SC.activation(T.hic[:, p0:p0 + n], T.sM[:, a + 15:z:16], AF.Abs), [("sM", c)], [("hic", c)])
            act(n, lambda a=a, z=z, l0=l0, l1=l1: SC.activation(T.lh[:, l0:l1], T.sm[:, a + 15:z:16], AF.Ln), [("sm", c)], [("lh", "xl", c)])
            act(n, lambda l1=l1, l2=l2, p0=p0, n=n: SC.activation(T.lh[:, l1:l2], T.hic[:, p0:p0 + n], AF.Ln), [("hic", c)], [("lh", "xh", c)])
            vec(2 * n, lambda l0=l0, l2=l2: V.tensor_scalar(T.LH[:, l0:l2], T.lh[:, l0:l2], 1.0 / H, float(N0 - 1), OP.mult, OP.add), [("lh", "xl", c), ("lh", "xh", c)], [("LH", c)])
            for nm, q0, q1 in (("xh", l1, l2), ("xl", l0, l1)):
                def gx(e, nm=nm, q0=q0, q1=q1, a=a, z=z, B=B):
                    src = T.X[:, 0:N0 + B].indirect(T.LH[:, q0:q1])
                    if e == "V":
                        return [V.tensor_copy(T[nm][:, a:z], src)]
                    return [SC.activation(T[nm][:, a:z], src, AF.Copy)]
                add("VS", w * GAT * CYC + 0.06, gx, [("LH", c)] + Xk, [(nm, c)])
            dk = []
            for s in range(a, z, 512):
                e_ = min(s + 512, z)
                if (c, (s - a) // 512) in DV:
                    vec(2 * (e_ - s), lambda s=s, e_=e_: V.tensor_tensor(T.df[:, s:e_], T.xl[:, s:e_], T.xh[:, s:e_], OP.subtract), [("xl", c), ("xh", c)], [("df", s)])
                    act(e_ - s, lambda s=s, e_=e_: SC.activation(T.da[:, s:e_], T.df[:, s:e_], AF.Abs), [("df", s)], [("da", s)])
                else:
                    bk = dfb % 4
                    dfb += 1
                    mm(e_ - s, lambda s=s, e_=e_, bk=bk: [PE.matmul(ps[bk][:, 0:e_ - s], T.NI[:], T.xh[:, s:e_], True, False)], ["NI", ("xh", c)], ["b%d" % bk])
                    mm(e_ - s, lambda s=s, e_=e_, bk=bk: [PE.matmul(ps[bk][:, 0:e_ - s], T.ID[:], T.xl[:, s:e_], False, True)], ["ID", ("xl", c)], ["b%d" % bk])
                    act(e_ - s, lambda s=s, e_=e_, bk=bk: SC.activation(T.da[:, s:e_], ps[bk][:, 0:e_ - s], AF.Abs), [], ["b%d" % bk, ("da", s)])
                dk.append(("da", s))

            def dm(a=a, z=z, p0=p0, n=n):
                return [PE.matmul(ps[4][:, p0:p0 + n], T.ZP[:, 15 - p:143 - p], T.da[:, a + p:z:16], p == 0, p == 15) for p in range(16)]
            mm(16 * max(64, n), dm, ["ZP"] + dk, ["b4"])
            vec(w / 2, lambda a=a, z=z, w=w: V.tensor_tensor_scan(T.sl[:, a:z], T.rmax[:, 0:w], T.xl[:, a:z], 0.0, OP.min, OP.max), ["rmax", ("xl", c)], [("sl", c)])
            vec(w / 2, lambda a=a, z=z, w=w: V.tensor_tensor_scan(T.sh[:, a:z], T.rmin[:, 0:w], T.xh[:, a:z], 0.0, OP.max, OP.min), ["rmin", ("xh", c)], [("sh", c)])
        lim = "lim" if t else "tauf"
        vec(NP, lambda lim=lim: V.tensor_scalar(T.far[:], ps[4][:, 0:NP], T[lim][:, 0:1], None, OP.is_gt), [lim], ["b4", ("far", 0)])

        def xm():
            o = ps[7][:, 0:NP]
            return [PE.matmul(o, T.HI[:], T.mh[:], True, False),
                    PE.matmul(o, T.HI[:], T.sl[:, 15:16 * NP:16], False, False),
                    PE.matmul(o, T.HI[:], T.sh[:, 15:16 * NP:16], False, True)]
        mm(3 * NP, xm, ["HI", "mh"] + [(k, c) for c in range(NCH) for k in ("sl", "sh")], ["b7"])
        vec(NP, lambda B=B: V.tensor_scalar(T.X[:, B:B + NP], ps[7][:, 0:NP], MAGIC, MAGIC, OP.add, OP.subtract), [], ["b7", "Xgap", ("X", t, 0)])
        m = 12
        mm(NP, lambda: [PE.matmul(ps[6][:, 128:128 + NP], T.BO[:], T.far[:], True, True)], ["BO", ("far", 0)], ["b6"])
        vec(NP, lambda: V.tensor_tensor(T.cm[:], ps[6][:, 128:128 + NP], T.msk[:], OP.is_gt), ["msk"], ["b6", "cm"])
        vec(NP / 2, lambda: V.tensor_tensor_scan(T.cs[:], T.rmax[:, 0:NP], T.cm[:], 0.0, OP.min, OP.max), ["rmax", "cm"], ["cs"])
        F = T.cs[:, 15:NP:16]
        vec(m, lambda F=F: V.tensor_tensor_scan(T.inc[:, 0:m], F, T.z12[:, 0:m], 0.0, OP.add, OP.max), ["z12", "cs"], [("inc", 0)])
        vec(2 * m, lambda F=F: V.tensor_tensor(T.Fw[:, 0:m], F, T.wc[:, 0:m], OP.mult), ["wc", "cs"], [("Fw", 0)])
        o6 = ps[6][:, 32:32 + m]
        mm(128, lambda F=F, o6=o6: [PE.matmul(o6, T.ID[:], T.wc[:, 0:m], True, False), PE.matmul(o6, T.TM[:], F, False, False)], ["ID", "TM", "wc", "cs"], ["b6"])
        mm(64, lambda o6=o6: [PE.matmul(o6, T.BO[:], T.inc[:, 0:m], False, False)], ["BO", ("inc", 0)], ["b6"])
        mm(64, lambda o6=o6: [PE.matmul(o6, T.NI[:], T.Fw[:, 0:m], False, True)], ["NI", ("Fw", 0)], ["b6"])
        vec(m, lambda o6=o6: V.tensor_scalar(T.slots[:, 0:m], o6, -1.0, None, OP.add), [], ["b6", ("slots", 0)])
        vec(3.5 * NP, lambda B=B, t=t: V.tensor_copy(T["mail%d" % t][:, 0:MW].indirect(T.slots[:, 0:m]), T.X[:, B:B + NP]), [("slots", 0), ("X", t, 0)], [("mail", t)])
        scat = lastw[("mail", t)]
        dst = T.cores[(rank + 1 + t % (len(T.cores) - 1)) % len(T.cores)]
        eng = topo.engines(core, dst)[:8]
        msk = sum(1 << e for e in eng)
        rid, pid = topo.addr(dst)[:2]
        ne = len(eng)
        m0, m1 = B + NP, B + G
        snd = add("G", 1.0, lambda e, t=t, rid=rid, pid=pid, msk=msk: [g.remote_dma(T["min%d" % t][:], T["mail%d" % t][:, 0:CAP], T.sem["arr%d" % t], T.sem.sent, pid, rid, msk)],
                  [("mail", t)], [], sem="sent", val=ne)
        arr = add("R", 0.0, None, [], [("min", t)], lat=MAILT, sem="arr%d" % t, val=ne, after=[snd])
        if t < RO - 1:
            def cp(a, b, src, rd):
                gps(0.2 + 2 * (b - a) * CYC, lambda: g.affine_select(T.X[:, a:b], src, [[0, b - a]], OP.is_equal, 0.0, 0, 0), rd, ["Xgap"])
            cp(N0 + B, N0 + B + NP, T.X[:, B:B + NP], [("X", t, 0), ("mail", t)])
            cp(m0, m1, T["min%d" % t][:], [("min", t)])
            cp(N0 + m0, N0 + m1, T["min%d" % t][:], [("min", t)])
        nl = [(k, c) for c in range(NCH) for k in ("sM", "sm")]
        mm(NP, lambda j0=j0: [PE.matmul(ps[5][:, 0:NP], T.ID[:], T.en[:, j0:j0 + NP], True, True)], ["ID", ("en", t)], ["b5"])
        vec(NP, lambda: V.tensor_tensor(T.fn[:], ps[5][:, 0:NP], T.far[:], OP.mult), [("far", 0)], ["b5", "fn"])
        act(NP, lambda: SC.activation(T.nrm[:], T.sM[:, 15:16 * NP:16], AF.Sign), nl, ["nrm"])
        act(NP, lambda: SC.activation(ps[0][:, 0:NP], T.nrm[:], AF.Relu), ["nrm"], ["b0"])
        act(NP, lambda: SC.activation(T.c0[:], T.sM[:, 15:16 * NP:16], AF.Relu, scale=-2.0 ** -WB), nl, ["c0"])
        vec(NP, lambda: V.tensor_tensor(T.loc[:], ps[0][:, 0:NP], T.sm[:, 15:16 * NP:16], OP.mult), nl, ["b0", "loc"])

        def ls():
            o = ps[5][:, 256:256 + NP]
            return [PE.matmul(o, T.ID[:], T.loc[:], True, False), PE.matmul(o, T.ID[:], T.c0[:], False, True)]
        mm(2 * NP, ls, ["ID", "c0", "loc"], ["b5"])
        vec(NP, lambda j0=j0: V.tensor_tensor(T.en[:, j0:j0 + NP], ps[5][:, 256:256 + NP], T.fn[:], OP.max), ["fn"], ["b5", ("en", t)])
        act(NP, lambda j0=j0: SC.activation(T.ln1[:], T.en[:, j0:j0 + NP], AF.Ln), [("en", t)], ["ln1"])
        act(NP, lambda: SC.activation(T.ln2[:], T.ln1[:], AF.Identity, bias=MAGIC + N0 - 1, scale=1.0 / H), ["ln1"], ["ln2"])
        act(NP, lambda j0=j0: SC.activation(T.A[:, j0:j0 + NP], T.ln2[:], AF.Identity, bias=-MAGIC), ["ln2"], [("A", t)])
        if t < RO - 1:
            kids(t + 1)
            vec(NP / 2, lambda B=B: V.tensor_scalar(T.f0[:, 0:NP], T.X[:, B:B + NP], T.thf[:, 0:1], -PLAIN, OP.is_lt, OP.mult), [("X", t, 0), "thf"], ["f0p"])
            act(NP, lambda j0=j0: SC.activation(T.ng[:, j0:j0 + NP], T.en[:, j0:j0 + NP], AF.Copy, scale=-2.0 ** WB), [("en", t)], [("ngp", t)])

            def ws(j0=j0):
                o = ps[4][:, 256:256 + NP]
                return [PE.matmul(o, T.ID[:], T.en[:, j0:j0 + NP], True, False), PE.matmul(o, T.ID[:], T.f0[:, 0:NP], False, True)]
            mm(2 * NP, ws, ["ID", ("en", t), "f0p"], ["b4"])
            vec(NP, lambda B=B, j0=j0: V.tensor_tensor(T.W[:, TOT + B:TOT + B + NP], ps[4][:, 256:256 + NP], T.ng[:, j0:j0 + NP], OP.max), [("ngp", t)], ["b4", ("W", t, "1p")])
            act(NP, lambda B=B: SC.activation(T.W[:, B:B + NP], ps[4][:, 256:256 + NP], AF.Copy), [], ["b4", ("W", t, "0p")])
            vec(CAP / 2, lambda t=t: V.tensor_scalar(T.f0[:, NP:G], T["min%d" % t][:], T.thf[:, 0:1], -PLAIN, OP.is_lt, OP.mult), [("min", t), "thf"], ["f0m"])
            add("V", 2 * CAP * CYC + FIX["V"], lambda e, B=B, j0=j0: [V.tensor_tensor(T.W[:, B + NP:B + G], T.en[:, j0 + NP:j0 + G], T.f0[:, NP:G], OP.add)],
                [("en", t), "f0m"], [("W", t, "0m")], after=gks)
            vec(2 * CAP, lambda B=B, j0=j0: V.tensor_tensor(T.W[:, TOT + B + NP:TOT + B + G], T.ng[:, j0 + NP:j0 + G], T.W[:, B + NP:B + G], OP.max),
                [("ngm", t), ("W", t, "0m")], [("W", t, "1m")])
            Wk += [("W", t, k) for k in ("0p", "1p", "0m", "1m")]
            Xk += [("X", t, 0)]

            def cc():
                return [PE.matmul(ps[6][:, 64:65], T.ones[:, 0:128], T.inc[:, 11:12], True, True),
                        PE.matmul(ps[6][:, 66:67], T.o16[:], T.inc[:, 11:12], True, False),
                        PE.matmul(ps[6][:, 66:67], T.ones[:, 0:128], T.q15[:, 0:1], False, True)]
            mm(192, cc, ["ones", "o16", "q15", ("inc", 0)], ["b6"])
            own(t + 1, [arr], [scat])
            act(1, lambda: SC.activation(T.cf[:], ps[6][:, 66:67], AF.Identity, bias=MAGIC), [], ["b6", "cf"])
            act(1, lambda: SC.activation(T.tc[:], ps[6][:, 64:65], AF.Identity, bias=T.tauf[:, 0:1]), ["tauf"], ["b6", "tc"])
            act(1, lambda: SC.activation(T.cg[:], T.cf[:], AF.Identity, bias=-MAGIC), ["cf"], ["cg"])
            act(1, lambda: SC.activation(T.lim[:], T.cg[:], AF.Identity, bias=T.tc[:, 0:1], scale=-16.0), ["cg", "tc"], ["lim"])
        dma(T.yx[:, j0:j0 + NP], T.X[:, B:B + NP], [("X", t, 0)], [])
        dma(T.ya[:, j0:j0 + G], T.A[:, j0:j0 + G], [("A", t)], [])
        dma(T.yx[:, j0 + NP:j0 + G], T["min%d" % t][:], [("min", t)], [])
    emit_all(g, T, tasks)


def plan(tasks):
    nt = len(tasks)
    succ = [[] for _ in range(nt)]
    for i, k in enumerate(tasks):
        for d in k["deps"]:
            succ[d].append(i)
    prio = [0.0] * nt
    for i in range(nt - 1, -1, -1):
        prio[i] = tasks[i]["cost"] + tasks[i]["lat"] + max([prio[s] + WAKE for s in succ[i]], default=0.0)
    left = [len(k["deps"]) for k in tasks]
    ready = [0.0] * nt
    free = {"V": 0.0, "S": 0.0, "P": 0.0, "G": 0.0, "Y": 0.0, "R": 0.0}
    avail = {i for i in range(nt) if left[i] == 0}
    where, seq = [None] * nt, []
    for i in range(nt):
        prio[i] += PRI.get(tasks[i]["lab"], 0.0)
    while avail:
        cand = []
        for i in avail:
            for q in tasks[i]["eng"]:
                st = ready[i] if q == "R" else max(free[q], ready[i])
                cand.append((st, -prio[i], i, q))
        first = min(cand)
        _, i, q, st = min((x[1], x[2], x[3], x[0]) for x in cand if x[3] == first[3] and x[0] <= first[0] + SLACK)
        avail.discard(i)
        k = tasks[i]
        end = st + k["cost"]
        if q != "R":
            free[q] = end
        where[i] = q
        seq.append(i)
        for s in succ[i]:
            ready[s] = max(ready[s], end + k["lat"] + WAKE)
            left[s] -= 1
            if left[s] == 0:
                avail.add(s)
    return where, seq, max(free.values())


def emit_all(g, T, tasks):
    where, seq, _ = plan(tasks)
    nt = len(tasks)
    at = [0] * nt
    for n, i in enumerate(seq):
        at[i] = n
    queues = {"V": g.vector, "S": g.scalar, "P": g.tensor, "G": g, "Y": g.sync}
    count = {}
    seen = {q: {} for q in queues}
    own = [None] * nt
    clock = [None] * nt
    for i in seq:
        k, q = tasks[i], where[i]
        if q == "R":
            own[i] = (k["sem"], k["val"])
            clock[i] = {k["sem"]: k["val"]}
            count[k["sem"]] = k["val"]
            continue
        for d in sorted(k["deps"], key=lambda d: -at[d]):
            s, v = own[d]
            if seen[q].get(s, 0) < v:
                queues[q].wait_ge(T.sem[s], v)
                for s2, v2 in clock[d].items():
                    seen[q][s2] = max(seen[q].get(s2, 0), v2)
        out = k["emit"](q)
        s = k["sem"] or "c" + q
        n = k["val"] if k["sem"] else 1
        for ins in out:
            if s != "sent":
                ins.then_inc(T.sem[s], n)
            count[s] = count.get(s, 0) + n
        own[i] = (s, count[s])
        clock[i] = dict(seen[q])
        clock[i][s] = count[s]
    for s in sorted(count):
        if seen["G"].get(s, 0) < count[s]:
            g.wait_ge(T.sem[s], count[s])
